import numpy as np
import ml_dtypes


def mxq(x, axis, fmt="e4m3"):
    dtype, down = {"e4m3": (ml_dtypes.float8_e4m3fn, 7), "e5m2": (ml_dtypes.float8_e5m2, 14)}[fmt]
    v = np.moveaxis(np.asarray(x, np.float32).astype(ml_dtypes.bfloat16).astype(np.float64), axis, -1)
    blocks = v.reshape(v.shape[:-1] + (-1, 32))
    amax = np.abs(blocks).max(-1, keepdims=True)
    byte = np.maximum(np.where(amax > 0, np.frexp(amax)[1] - 1 + 127, 0) - down, 1)
    scale = np.exp2(byte - 127.0)
    codes = (blocks / scale).astype(np.float32).astype(dtype).astype(np.float64)
    return np.moveaxis((codes * scale).reshape(v.shape), -1, axis)


WIDE = False


def mx_kscale(k):
    if not WIDE:
        return np.ones(k)
    levels = np.array([30, -30])
    if k % 512:
        return np.exp2(np.random.permutation(np.resize(levels, k // 32))).repeat(32)
    a = np.empty((k // 512, 16))
    for p in range(k // 512):
        a[p, :8] = np.random.permutation(np.resize(levels, 8))
        for g in range(8):
            far = levels[np.abs(levels - a[p, g]) >= 10]
            a[p, g + 8] = far[np.random.randint(len(far))]
    return np.exp2(a.ravel()).repeat(32)


BF16 = ml_dtypes.bfloat16


def bf(x):
    return np.asarray(x, np.float32).astype(BF16)


def f64(x):
    return np.asarray(x).astype(np.float64)


E2M1 = np.array([0.0, 0.5, 1.0, 1.5, 2.0, 3.0, 4.0, 6.0, -0.0, -0.5, -1.0, -1.5, -2.0, -3.0, -4.0, -6.0])


def pack_weight(w, fmt):
    k, n = w.shape
    w = f64(bf(w)).reshape(k // 32, 32, n)
    amax = np.abs(w).max(1)
    if fmt in ("e4m3", "e5m2"):
        byte = np.frexp(amax)[1] - 1 + 127 - (7 if fmt == "e4m3" else 14)
    else:
        mant, ex = np.frexp(amax / 6.0)
        byte = np.where(mant > 0.5, ex, ex - 1) + 127
    byte = np.clip(np.where(amax > 0, byte, 1), 1, 254)
    scaled = (w * np.exp2(127.0 - byte)[:, None, :]).reshape(k, n).astype(np.float32)
    by_word = np.ascontiguousarray(scaled.reshape(k // 512, 128, 4, n).transpose(0, 1, 3, 2))
    if fmt in ("e4m3", "e5m2"):
        words = by_word.astype(ml_dtypes.float8_e4m3fn if fmt == "e4m3" else ml_dtypes.float8_e5m2).view(np.uint8)
    else:
        c = by_word.astype(ml_dtypes.float4_e2m1fn).view(np.uint8) & 0xF
        words = c[..., 0::2] | (c[..., 1::2] << 4)
    return np.ascontiguousarray(words), np.ascontiguousarray(byte.astype(np.uint8).reshape(k // 512, 16, n))


def unpack_weight(words, scales, fmt):
    g, p, n, _ = words.shape
    if fmt in ("e4m3", "e5m2"):
        vals = np.ascontiguousarray(words).view(ml_dtypes.float8_e4m3fn if fmt == "e4m3" else ml_dtypes.float8_e5m2).astype(np.float64)
    else:
        nib = np.empty((g, p, n, 4), np.uint8)
        nib[..., 0::2] = words & 0xF
        nib[..., 1::2] = words >> 4
        vals = E2M1[nib]
    vals = vals * np.repeat(np.exp2(scales.astype(np.float64) - 127.0), 8, axis=1)[..., None]
    return vals.transpose(0, 1, 3, 2).reshape(g * 512, n)


C, D, L, B = 1024, 2048, 512, 1024


def setup_inputs():
    s = mx_kscale(C)
    t = mx_kscale(D)
    G = 0.6 * np.random.standard_normal((C, B)) * np.exp(0.7 * np.random.standard_normal((C, B)))
    g_words, g_scales = pack_weight(G * s[:, None], "e5m2")
    return {"g_words": g_words, "g_scales": g_scales,
            "a": bf(np.random.standard_normal((C, D)) / np.sqrt(C) / s[:, None] * t),
            "cost": bf(0.5 * np.random.standard_normal(D) * t),
            "slope": bf(1.0 - np.tanh(np.random.standard_normal((D, B))) ** 2),
            "w": bf(np.random.standard_normal((D, L)) / np.sqrt(D) / t[:, None]),
            "tau": bf(0.3 + 0.1 * np.abs(np.random.standard_normal(L))),
            "z": bf(np.random.standard_normal((L, B)))}


def reference(g_words, g_scales, a, cost, slope, w, tau, z):
    G = unpack_weight(g_words, g_scales, "e5m2")
    ag = mxq(f64(a), 0, "e4m3").T @ G
    h = (ag + f64(cost)[:, None]) * f64(slope)
    wh = mxq(f64(w), 0, "e4m3").T @ mxq(h, 0, "e5m2")
    return wh + f64(tau)[:, None] * f64(z)

@@ -1,0 +1,248 @@
+from contextlib import ExitStack
+
+import concourse.mybir as mybir
+
+C, D, L, B = 1024, 2048, 512, 1024
+FLOPS = 2 * C * D * B + 2 * D * L * B
+
+F32 = mybir.dt.float32
+BF16 = mybir.dt.bfloat16
+I32 = mybir.dt.int32
+U32 = mybir.dt.uint32
+U8 = mybir.dt.uint8
+E4M3 = mybir.dt.float8_e4m3fn_x4
+E5M2 = mybir.dt.float8_e5m2_x4
+ADD = mybir.AluOpType.add
+MULT = mybir.AluOpType.mult
+
+P = 128
+PACK = 4
+K = P * PACK
+N = 512
+GROUPS = C // K
+CHUNKS = D // K
+HALVES = B // N
+
+TILES = [(0, 0), (1, 0), (0, 1), (1, 1), (2, 0), (3, 0), (2, 1), (3, 1)]
+
+HEAD = [("w", 0), ("a", 0, 0), ("a", 1, 0), ("w", 1), ("a", 0, 1), ("a", 1, 1), ("a", 2, 0)]
+BESIDE = {0: [("a", 3, 0)], 2: [("a", 2, 1)], 3: [("a", 3, 1)], 4: [("w", 2)], 5: [("w", 3)]}
+
+
+def tile_augmented_lagrangian_latent_gradient_e3_kernel(
+    tc, g_words, g_scales, a, cost, slope, w, tau, z, out
+):
+    nc = tc.nc
+    with ExitStack() as ctx:
+        keep = ctx.enter_context(tc.tile_pool(name="keep", bufs=1))
+        stage = ctx.enter_context(tc.tile_pool(name="stage", bufs=3))
+        psum = ctx.enter_context(tc.psum_pool(name="psum", bufs=1))
+        ctx.enter_context(tc.manual_schedule())
+
+        def sbuf(name, shape, dtype):
+            return keep.tile(shape, dtype, name=name, align_bytes=64)
+
+        g_codes = [sbuf("g_codes%d" % h, [P, GROUPS, N], U32) for h in range(HALVES)]
+        g_planes = sbuf("g_planes", [P, GROUPS, B], U8)
+        a_raw = [[sbuf("a_raw%d%d" % (q, g), [P, PACK, D // 2], BF16) for g in range(GROUPS)] for q in range(2)]
+        a_codes = [[sbuf("a_codes%d%d" % (c, g), [P, K], U32) for g in range(GROUPS)] for c in range(CHUNKS)]
+        a_planes = [[sbuf("a_planes%d%d" % (c, g), [P, K], U8) for g in range(GROUPS)] for c in range(CHUNKS)]
+        slopes = [sbuf("slopes%d" % c, [P, PACK, B], BF16) for c in range(CHUNKS)]
+        w_raw = [sbuf("w_raw%d" % c, [P, PACK, L], BF16) for c in range(CHUNKS)]
+        w_codes = [sbuf("w_codes%d" % c, [P, L], U32) for c in range(CHUNKS)]
+        w_planes = [sbuf("w_planes%d" % c, [P, L], U8) for c in range(CHUNKS)]
+        h_codes = {tile: sbuf("h_codes%d%d" % tile, [P, N], U32) for tile in TILES}
+        h_planes = {tile: sbuf("h_planes%d%d" % tile, [P, N], U8) for tile in TILES}
+        costs = sbuf("costs", [P, CHUNKS, PACK], BF16)
+        taus = sbuf("taus", [P, PACK], BF16)
+        z_rows = sbuf("z_rows", [P, PACK, B], BF16)
+
+        def load_a(q, g):
+            source = a[K * g : K * (g + 1), q * (D // 2) : (q + 1) * (D // 2)]
+            nc.sync.dma_start(out=a_raw[q][g][:], in_=source.rearrange("(p j) d -> p j d", j=PACK))
+
+        def load_g(h):
+            source = g_words.rearrange("g p n t -> p g (n t)")[:, :, PACK * N * h : PACK * N * (h + 1)]
+            nc.sync.dma_start(out=g_codes[h][:].bitcast(I32), in_=source.bitcast(I32))
+
+        def load_g_planes():
+            source = g_scales.bitcast(I32)
+            for q in range(4):
+                nc.sync.dma_start(
+                    out=g_planes[32 * q : 32 * q + 4, :, :].bitcast(I32),
+                    in_=source[:, 4 * q : 4 * q + 4, :].rearrange("g r n -> r g n"),
+                )
+
+        def load_slope(c, columns):
+            source = slope[K * c : K * (c + 1), columns]
+            nc.sync.dma_start(out=slopes[c][:, :, columns], in_=source.rearrange("(p t) n -> p t n", t=PACK))
+
+        def load_w(c):
+            nc.sync.dma_start(out=w_raw[c][:], in_=w[K * c : K * (c + 1), :].rearrange("(p j) l -> p j l", j=PACK))
+
+        nc.vector.memset(g_planes[:].rearrange("p g n -> p (g n)").bitcast(U32), 0)
+
+        first_half, second_half, whole = slice(0, N), slice(N, B), slice(0, B)
+        load_w(0)
+        load_a(0, 0)
+        load_w(1)
+        load_a(0, 1)
+        load_g(0)
+        load_a(1, 0)
+        load_g_planes()
+        nc.sync.dma_start(out=costs[:], in_=cost.rearrange("(c p t) -> p c t", c=CHUNKS, t=PACK))
+        load_slope(0, first_half)
+        load_slope(1, whole)
+        load_g(1)
+        load_slope(0, second_half)
+        load_a(1, 1)
+        load_slope(2, whole)
+        nc.sync.dma_start(out=taus[:], in_=tau.rearrange("(p m) -> p m", m=PACK))
+        load_w(2)
+        load_slope(3, whole)
+        load_w(3)
+        nc.sync.dma_start(out=z_rows[:], in_=z.rearrange("(p m) n -> p m n", m=PACK))
+
+        grouped = {}
+
+        def interleave(x):
+            if x[0] == "a":
+                c, g = x[1], x[2]
+                source = a_raw[c // 2][g][:, :, K * (c % 2) : K * (c % 2 + 1)]
+            else:
+                source = w_raw[x[1]][:]
+            grouped[x] = stage.tile([P, K * PACK], BF16, name="grouped", align_bytes=64, bufs=5)
+            dst = grouped[x][:].rearrange("p (t m i j) -> p t m j i", t=PACK, i=2, j=PACK)
+            src = source.rearrange("p j (m i t) -> p t m j i", i=2, t=PACK)
+            pairs = K // PACK // 2
+            cut = 0 if x[:2] == ("a", CHUNKS - 1) else pairs // 2
+            if cut:
+                nc.vector.tensor_copy(out=dst[:, :, :cut], in_=src[:, :, :cut])
+            nc.scalar.copy(dst[:, :, cut:], src[:, :, cut:])
+
+        def quantise(x):
+            if x[0] == "a":
+                codes, planes = a_codes[x[1]][x[2]], a_planes[x[1]][x[2]]
+            else:
+                codes, planes = w_codes[x[1]], w_planes[x[1]]
+            nc.vector.quantize_mx(out=codes[:].bitcast(E4M3), scales=planes[:], in_=grouped[x][:])
+
+        banks = {}
+
+        def first_product(i, t, groups):
+            c, h = TILES[i]
+            columns = slice(P * t, P * (t + 1))
+            for g in groups:
+                if g == 0:
+                    banks[i, t] = psum.tile([P, N], F32, name="bank%d" % t)
+                nc.tensor.matmul_mx(
+                    out=banks[i, t][:],
+                    lhsT=a_codes[c][g][:, columns].bitcast(E4M3),
+                    lhsT_scale=a_planes[c][g][:, columns],
+                    rhs=g_codes[h][:, g, :].bitcast(E5M2),
+                    rhs_scale=g_planes[:, g, N * h : N * (h + 1)],
+                    start=(g == 0),
+                    stop=(g == GROUPS - 1),
+                )
+
+        h_rows, h_grouped = {}, {}
+
+        def read_banks(i):
+            c, h = TILES[i]
+            h_rows[i] = stage.tile([P, PACK, N], BF16, name="h_rows", align_bytes=64)
+            for t in range(PACK):
+                nc.vector.scalar_tensor_tensor(
+                    out=h_rows[i][:, t, :],
+                    in0=banks[i, t][:],
+                    scalar=costs[:, c, t : t + 1],
+                    in1=slopes[c][:, t, N * h : N * (h + 1)],
+                    op0=ADD,
+                    op1=MULT,
+                )
+
+        def interleave_h(i):
+            h_grouped[i] = stage.tile([P, N * PACK], BF16, name="h_grouped", align_bytes=64)
+            nc.scalar.copy(
+                h_grouped[i][:].rearrange("p (n i t) -> p n t i", i=4, t=PACK),
+                h_rows[i][:].rearrange("p t (n i) -> p n t i", i=4),
+            )
+
+        def quantise_h(i):
+            tile = TILES[i]
+            nc.vector.quantize_mx(out=h_codes[tile][:].bitcast(E5M2), scales=h_planes[tile][:], in_=h_grouped[i][:])
+
+        sums = {}
+
+        def second_product(c, h, m):
+            columns = slice(P * m, P * (m + 1))
+            nc.tensor.matmul_mx(
+                out=sums[h, m][:],
+                lhsT=w_codes[c][:, columns].bitcast(E4M3),
+                lhsT_scale=w_planes[c][:, columns],
+                rhs=h_codes[c, h][:].bitcast(E5M2),
+                rhs_scale=h_planes[c, h][:],
+                start=(c == 0),
+                stop=(c == CHUNKS - 1),
+            )
+
+        out_rows = out.rearrange("(p m) n -> p m n", m=PACK)
+
+        def finish(h, m):
+            columns = slice(N * h, N * (h + 1))
+            result = stage.tile([P, N], F32, name="result", align_bytes=64, bufs=8)
+            nc.vector.scalar_tensor_tensor(
+                out=result[:],
+                in0=z_rows[:, m, columns],
+                scalar=taus[:, m : m + 1],
+                in1=sums[h, m][:],
+                op0=MULT,
+                op1=ADD,
+            )
+            nc.sync.dma_start(out=out_rows[:, m, columns], in_=result[:])
+
+        for x, before in zip(HEAD, [None] + HEAD):
+            interleave(x)
+            if before:
+                quantise(before)
+        quantise(HEAD[-1])
+        for g in range(GROUPS):
+            for t in range(PACK):
+                first_product(0, t, [g])
+        for m in range(PACK):
+            sums[0, m] = psum.tile([P, N], F32, name="sum%d" % m)
+
+        last = len(TILES) - 1
+        ready = set(HEAD)
+        summed = 0
+        for i in range(last + 1):
+            read_banks(i)
+            for x in BESIDE.get(i, []):
+                interleave(x)
+            if i < last:
+                interleave_h(i)
+            for x in BESIDE.get(i - 1, []):
+                quantise(x)
+                ready.add(x)
+            if i < last:
+                for t in range(PACK):
+                    first_product(i + 1, t, range(GROUPS))
+            if i > 0:
+                quantise_h(i - 1)
+                ready.add(TILES[i - 1])
+            while summed < CHUNKS and ("w", summed) in ready and (summed, 0) in ready:
+                for m in range(PACK):
+                    second_product(summed, 0, m)
+                summed += 1
+
+        for m in range(PACK):
+            finish(0, m)
+        interleave_h(last)
+        for m in range(PACK):
+            sums[1, m] = psum.tile([P, N], F32, name="bank%d" % m)
+        for c in range(CHUNKS):
+            if c == CHUNKS - 1:
+                quantise_h(last)
+            for m in range(PACK):
+                second_product(c, 1, m)
+        for m in range(PACK):
+            finish(1, m)

@@ -23,10 +23,12 @@ GROUPS = C // K
 CHUNKS = D // K
 HALVES = B // N
 
-TILES = [(0, 0), (1, 0), (0, 1), (1, 1), (2, 0), (3, 0), (2, 1), (3, 1)]
+TILES = [(c, h) for c in range(CHUNKS) for h in range(HALVES)]
 
-HEAD = [("w", 0), ("a", 0, 0), ("a", 1, 0), ("w", 1), ("a", 0, 1), ("a", 1, 1), ("a", 2, 0)]
-BESIDE = {0: [("a", 3, 0)], 2: [("a", 2, 1)], 3: [("a", 3, 1)], 4: [("w", 2)], 5: [("w", 3)]}
+QUEUE = [("a", 1, 0), ("a", 1, 1), ("a", 2, 0), ("a", 2, 1), ("w", 0), ("a", 3, 0), ("a", 3, 1),
+         ("w", 1), ("w", 2), ("w", 3)]
+SLOTS = [4, 4, 6, 6, 6, 5, 5, 4]
+POOL_SHARE = 96
 
 
 def tile_augmented_lagrangian_latent_gradient_e3_kernel(
@@ -44,10 +46,10 @@ def tile_augmented_lagrangian_latent_gradient_e3_kernel(
 
         g_codes = [sbuf("g_codes%d" % h, [P, GROUPS, N], U32) for h in range(HALVES)]
         g_planes = sbuf("g_planes", [P, GROUPS, B], U8)
-        a_raw = [[sbuf("a_raw%d%d" % (q, g), [P, PACK, D // 2], BF16) for g in range(GROUPS)] for q in range(2)]
+        a_raw = [[sbuf("a_raw%d%d" % (c, g), [P, PACK, K], BF16) for g in range(GROUPS)] for c in range(CHUNKS)]
         a_codes = [[sbuf("a_codes%d%d" % (c, g), [P, K], U32) for g in range(GROUPS)] for c in range(CHUNKS)]
         a_planes = [[sbuf("a_planes%d%d" % (c, g), [P, K], U8) for g in range(GROUPS)] for c in range(CHUNKS)]
-        slopes = [sbuf("slopes%d" % c, [P, PACK, B], BF16) for c in range(CHUNKS)]
+        slopes = {tile: sbuf("slopes%d%d" % tile, [P, PACK, N], BF16) for tile in TILES}
         w_raw = [sbuf("w_raw%d" % c, [P, PACK, L], BF16) for c in range(CHUNKS)]
         w_codes = [sbuf("w_codes%d" % c, [P, L], U32) for c in range(CHUNKS)]
         w_planes = [sbuf("w_planes%d" % c, [P, L], U8) for c in range(CHUNKS)]
@@ -57,115 +59,113 @@ def tile_augmented_lagrangian_latent_gradient_e3_kernel(
         taus = sbuf("taus", [P, PACK], BF16)
         z_rows = sbuf("z_rows", [P, PACK, B], BF16)
 
-        def load_a(q, g):
-            source = a[K * g : K * (g + 1), q * (D // 2) : (q + 1) * (D // 2)]
-            nc.sync.dma_start(out=a_raw[q][g][:], in_=source.rearrange("(p j) d -> p j d", j=PACK))
-
-        def load_g(h):
-            source = g_words.rearrange("g p n t -> p g (n t)")[:, :, PACK * N * h : PACK * N * (h + 1)]
-            nc.sync.dma_start(out=g_codes[h][:].bitcast(I32), in_=source.bitcast(I32))
-
-        def load_g_planes():
-            source = g_scales.bitcast(I32)
-            for q in range(4):
-                nc.sync.dma_start(
-                    out=g_planes[32 * q : 32 * q + 4, :, :].bitcast(I32),
-                    in_=source[:, 4 * q : 4 * q + 4, :].rearrange("g r n -> r g n"),
-                )
-
-        def load_slope(c, columns):
-            source = slope[K * c : K * (c + 1), columns]
-            nc.sync.dma_start(out=slopes[c][:, :, columns], in_=source.rearrange("(p t) n -> p t n", t=PACK))
-
-        def load_w(c):
-            nc.sync.dma_start(out=w_raw[c][:], in_=w[K * c : K * (c + 1), :].rearrange("(p j) l -> p j l", j=PACK))
+        def load(x):
+            if x[0] == "a":
+                c, g = x[1], x[2]
+                source = a[K * g : K * (g + 1), K * c : K * (c + 1)]
+                nc.sync.dma_start(out=a_raw[c][g][:], in_=source.rearrange("(p j) d -> p j d", j=PACK))
+            elif x[0] == "w":
+                c = x[1]
+                source = w[K * c : K * (c + 1), :]
+                nc.sync.dma_start(out=w_raw[c][:], in_=source.rearrange("(p j) l -> p j l", j=PACK))
+            elif x[0] == "g":
+                h = x[1]
+                source = g_words.rearrange("g p n t -> p g (n t)")[:, :, PACK * N * h : PACK * N * (h + 1)]
+                nc.sync.dma_start(out=g_codes[h][:].bitcast(I32), in_=source.bitcast(I32))
+            else:
+                c, h = x[1], x[2]
+                source = slope[K * c : K * (c + 1), N * h : N * (h + 1)]
+                nc.sync.dma_start(out=slopes[c, h][:], in_=source.rearrange("(p t) n -> p t n", t=PACK))
 
         nc.vector.memset(g_planes[:].rearrange("p g n -> p (g n)").bitcast(U32), 0)
 
-        first_half, second_half, whole = slice(0, N), slice(N, B), slice(0, B)
-        load_w(0)
-        load_a(0, 0)
-        load_w(1)
-        load_a(0, 1)
-        load_g(0)
-        load_a(1, 0)
-        load_g_planes()
-        nc.sync.dma_start(out=costs[:], in_=cost.rearrange("(c p t) -> p c t", c=CHUNKS, t=PACK))
-        load_slope(0, first_half)
-        load_slope(1, whole)
-        load_g(1)
-        load_slope(0, second_half)
-        load_a(1, 1)
-        load_slope(2, whole)
+        load(("a", 0, 0))
+        load(("a", 0, 1))
+        for q in range(4):
+            nc.scalar.dma_start(
+                out=g_planes[32 * q : 32 * q + 4, :, :].bitcast(I32),
+                in_=g_scales.bitcast(I32)[:, 4 * q : 4 * q + 4, :].rearrange("g r n -> r g n"),
+            )
+        nc.scalar.dma_start(out=costs[:], in_=cost.rearrange("(c p t) -> p c t", c=CHUNKS, t=PACK))
+        for x in [
+            ("g", 0), ("s", 0, 0), ("a", 1, 0), ("g", 1), ("s", 0, 1), ("a", 1, 1), ("s", 1, 0),
+            ("a", 2, 0), ("a", 2, 1), ("s", 1, 1), ("w", 0), ("a", 3, 0), ("s", 2, 0), ("a", 3, 1),
+            ("w", 1), ("s", 2, 1), ("w", 2), ("s", 3, 0), ("w", 3), ("s", 3, 1),
+        ]:
+            load(x)
         nc.sync.dma_start(out=taus[:], in_=tau.rearrange("(p m) -> p m", m=PACK))
-        load_w(2)
-        load_slope(3, whole)
-        load_w(3)
         nc.sync.dma_start(out=z_rows[:], in_=z.rearrange("(p m) n -> p m n", m=PACK))
 
         grouped = {}
 
-        def interleave(x):
-            if x[0] == "a":
-                c, g = x[1], x[2]
-                source = a_raw[c // 2][g][:, :, K * (c % 2) : K * (c % 2 + 1)]
+        def interleave(x, slots, engine):
+            source = a_raw[x[1]][x[2]][:] if x[0] == "a" else w_raw[x[1]][:]
+            if x not in grouped:
+                grouped[x] = stage.tile([P, K * PACK], BF16, name="grouped", align_bytes=64, bufs=3)
+            dst = grouped[x][:].rearrange("p (t m i j) -> p t m j i", t=PACK, i=2, j=PACK)[:, slots]
+            src = source.rearrange("p j (m i t) -> p t m j i", i=2, t=PACK)[:, slots]
+            if engine == "vector":
+                nc.vector.tensor_copy(out=dst, in_=src)
             else:
-                source = w_raw[x[1]][:]
-            grouped[x] = stage.tile([P, K * PACK], BF16, name="grouped", align_bytes=64, bufs=5)
-            dst = grouped[x][:].rearrange("p (t m i j) -> p t m j i", t=PACK, i=2, j=PACK)
-            src = source.rearrange("p j (m i t) -> p t m j i", i=2, t=PACK)
-            pairs = K // PACK // 2
-            cut = 0 if x[:2] == ("a", CHUNKS - 1) else pairs // 2
-            if cut:
-                nc.vector.tensor_copy(out=dst[:, :, :cut], in_=src[:, :, :cut])
-            nc.scalar.copy(dst[:, :, cut:], src[:, :, cut:])
+                nc.scalar.copy(dst, src)
 
-        def quantise(x):
+        def quantise(x, slots):
             if x[0] == "a":
                 codes, planes = a_codes[x[1]][x[2]], a_planes[x[1]][x[2]]
             else:
                 codes, planes = w_codes[x[1]], w_planes[x[1]]
-            nc.vector.quantize_mx(out=codes[:].bitcast(E4M3), scales=planes[:], in_=grouped[x][:])
+            columns = slice(P * slots.start, P * slots.stop)
+            nc.vector.quantize_mx(
+                out=codes[:, columns].bitcast(E4M3),
+                scales=planes[:, columns],
+                in_=grouped[x][:, K * slots.start : K * slots.stop],
+            )
 
         banks = {}
 
-        def first_product(i, t, groups):
+        def first_product(i, t, g):
             c, h = TILES[i]
             columns = slice(P * t, P * (t + 1))
-            for g in groups:
-                if g == 0:
-                    banks[i, t] = psum.tile([P, N], F32, name="bank%d" % t)
-                nc.tensor.matmul_mx(
-                    out=banks[i, t][:],
-                    lhsT=a_codes[c][g][:, columns].bitcast(E4M3),
-                    lhsT_scale=a_planes[c][g][:, columns],
-                    rhs=g_codes[h][:, g, :].bitcast(E5M2),
-                    rhs_scale=g_planes[:, g, N * h : N * (h + 1)],
-                    start=(g == 0),
-                    stop=(g == GROUPS - 1),
-                )
+            if g == 0:
+                banks[i, t] = psum.tile([P, N], F32, name="bank%d" % t)
+            nc.tensor.matmul_mx(
+                out=banks[i, t][:],
+                lhsT=a_codes[c][g][:, columns].bitcast(E4M3),
+                lhsT_scale=a_planes[c][g][:, columns],
+                rhs=g_codes[h][:, g, :].bitcast(E5M2),
+                rhs_scale=g_planes[:, g, N * h : N * (h + 1)],
+                start=(g == 0),
+                stop=(g == GROUPS - 1),
+            )
 
         h_rows, h_grouped = {}, {}
 
         def read_banks(i):
             c, h = TILES[i]
-            h_rows[i] = stage.tile([P, PACK, N], BF16, name="h_rows", align_bytes=64)
+            h_rows[i] = stage.tile([P, PACK, N], BF16, name="h_rows", align_bytes=64, bufs=2)
             for t in range(PACK):
                 nc.vector.scalar_tensor_tensor(
                     out=h_rows[i][:, t, :],
                     in0=banks[i, t][:],
                     scalar=costs[:, c, t : t + 1],
-                    in1=slopes[c][:, t, N * h : N * (h + 1)],
+                    in1=slopes[c, h][:, t, :],
                     op0=ADD,
                     op1=MULT,
                 )
 
         def interleave_h(i):
-            h_grouped[i] = stage.tile([P, N * PACK], BF16, name="h_grouped", align_bytes=64)
-            nc.scalar.copy(
-                h_grouped[i][:].rearrange("p (n i t) -> p n t i", i=4, t=PACK),
-                h_rows[i][:].rearrange("p t (n i) -> p n t i", i=4),
+            h_grouped[i] = stage.tile([P, N * PACK], BF16, name="h_grouped", align_bytes=64, bufs=1)
+            dst = h_grouped[i][:].rearrange("p (n i t) -> p n t i", i=4, t=PACK)
+            src = h_rows[i][:].rearrange("p t (n i) -> p n t i", i=4)
+            nc.gpsimd.tensor_scalar(
+                out=h_grouped[i][:].rearrange("p (n t) -> p n t", t=PACK)[:, : 4 * POOL_SHARE],
+                in0=h_rows[i][:].rearrange("p t n -> p n t")[:, : 4 * POOL_SHARE],
+                scalar1=1.0,
+                scalar2=0.0,
+                op0=MULT,
+                op1=ADD,
             )
+            nc.scalar.copy(dst[:, POOL_SHARE:], src[:, POOL_SHARE:])
 
         def quantise_h(i):
             tile = TILES[i]
@@ -173,7 +173,7 @@ def tile_augmented_lagrangian_latent_gradient_e3_kernel(
 
         sums = {}
 
-        def second_product(c, h, m):
+        def second_product(c, h, m, start, stop):
             columns = slice(P * m, P * (m + 1))
             nc.tensor.matmul_mx(
                 out=sums[h, m][:],
@@ -181,8 +181,8 @@ def tile_augmented_lagrangian_latent_gradient_e3_kernel(
                 lhsT_scale=w_planes[c][:, columns],
                 rhs=h_codes[c, h][:].bitcast(E5M2),
                 rhs_scale=h_planes[c, h][:],
-                start=(c == 0),
-                stop=(c == CHUNKS - 1),
+                start=start,
+                stop=stop,
             )
 
         out_rows = out.rearrange("(p m) n -> p m n", m=PACK)
@@ -200,49 +200,57 @@ def tile_augmented_lagrangian_latent_gradient_e3_kernel(
             )
             nc.sync.dma_start(out=out_rows[:, m, columns], in_=result[:])
 
-        for x, before in zip(HEAD, [None] + HEAD):
-            interleave(x)
-            if before:
-                quantise(before)
-        quantise(HEAD[-1])
         for g in range(GROUPS):
+            x = ("a", 0, g)
+            interleave(x, slice(0, 2), "vector")
+            interleave(x, slice(3, 4), "scalar")
+            interleave(x, slice(2, 3), "vector")
+            quantise(x, slice(0, 2))
+            quantise(x, slice(2, 4))
             for t in range(PACK):
-                first_product(0, t, [g])
+                first_product(0, t, g)
         for m in range(PACK):
             sums[0, m] = psum.tile([P, N], F32, name="sum%d" % m)
 
         last = len(TILES) - 1
-        ready = set(HEAD)
+        done = 0
+        ready = set()
         summed = 0
         for i in range(last + 1):
             read_banks(i)
-            for x in BESIDE.get(i, []):
-                interleave(x)
-            if i < last:
-                interleave_h(i)
-            for x in BESIDE.get(i - 1, []):
-                quantise(x)
-                ready.add(x)
-            if i < last:
-                for t in range(PACK):
-                    first_product(i + 1, t, range(GROUPS))
+            start, done = done, done + SLOTS[i]
+            for k in range(start // PACK, (done + PACK - 1) // PACK):
+                slots = slice(max(start - PACK * k, 0), min(done - PACK * k, PACK))
+                interleave(QUEUE[k], slots, "scalar")
+                if k == start // PACK and i > 0:
+                    interleave_h(i - 1)
+            for k in range(start // PACK, done // PACK):
+                quantise(QUEUE[k], slice(0, PACK))
+                ready.add(QUEUE[k])
             if i > 0:
                 quantise_h(i - 1)
                 ready.add(TILES[i - 1])
-            while summed < CHUNKS and ("w", summed) in ready and (summed, 0) in ready:
+            if i < last:
+                for g in range(GROUPS):
+                    for t in range(PACK):
+                        first_product(i + 1, t, g)
+            while summed < CHUNKS - 1 and ("w", summed) in ready and (summed, 0) in ready:
                 for m in range(PACK):
-                    second_product(summed, 0, m)
+                    second_product(summed, 0, m, summed == 0, False)
                 summed += 1
 
-        for m in range(PACK):
-            finish(0, m)
         interleave_h(last)
         for m in range(PACK):
             sums[1, m] = psum.tile([P, N], F32, name="bank%d" % m)
-        for c in range(CHUNKS):
-            if c == CHUNKS - 1:
-                quantise_h(last)
+            second_product(0, 1, m, True, False)
+        for c in range(summed, CHUNKS):
             for m in range(PACK):
-                second_product(c, 1, m)
+                second_product(c, 0, m, False, c == CHUNKS - 1)
+        for m in range(PACK):
+            finish(0, m)
+        quantise_h(last)
+        for c in range(1, CHUNKS):
+            for m in range(PACK):
+                second_product(c, 1, m, False, c == CHUNKS - 1)
         for m in range(PACK):
             finish(1, m)

@@ -25,10 +25,10 @@ HALVES = B // N
 
 TILES = [(c, h) for c in range(CHUNKS) for h in range(HALVES)]
 
-QUEUE = [("a", 1, 0), ("a", 1, 1), ("a", 2, 0), ("a", 2, 1), ("w", 0), ("a", 3, 0), ("a", 3, 1),
-         ("w", 1), ("w", 2), ("w", 3)]
-SLOTS = [4, 4, 6, 6, 6, 5, 5, 4]
-POOL_SHARE = 96
+QUEUE = [("a", 2, 0), ("a", 2, 1), ("w", 0), ("a", 3, 0), ("a", 3, 1), ("w", 1), ("w", 2), ("w", 3)]
+PIECES = {1: 1, 2: 3, 3: 2, 4: 3, 5: 2, 6: 3, 7: 2}
+POOL_SHARE = 416
+AHEAD = 1
 
 
 def tile_augmented_lagrangian_latent_gradient_e3_kernel(
@@ -55,7 +55,7 @@ def tile_augmented_lagrangian_latent_gradient_e3_kernel(
         w_planes = [sbuf("w_planes%d" % c, [P, L], U8) for c in range(CHUNKS)]
         h_codes = {tile: sbuf("h_codes%d%d" % tile, [P, N], U32) for tile in TILES}
         h_planes = {tile: sbuf("h_planes%d%d" % tile, [P, N], U8) for tile in TILES}
-        costs = sbuf("costs", [P, CHUNKS, PACK], BF16)
+        costs = [sbuf("costs0", [P, 1, PACK], BF16), sbuf("costs1", [P, CHUNKS - 1, PACK], BF16)]
         taus = sbuf("taus", [P, PACK], BF16)
         z_rows = sbuf("z_rows", [P, PACK, B], BF16)
 
@@ -69,9 +69,9 @@ def tile_augmented_lagrangian_latent_gradient_e3_kernel(
                 source = w[K * c : K * (c + 1), :]
                 nc.sync.dma_start(out=w_raw[c][:], in_=source.rearrange("(p j) l -> p j l", j=PACK))
             elif x[0] == "g":
-                h = x[1]
-                source = g_words.rearrange("g p n t -> p g (n t)")[:, :, PACK * N * h : PACK * N * (h + 1)]
-                nc.sync.dma_start(out=g_codes[h][:].bitcast(I32), in_=source.bitcast(I32))
+                h, groups = x[1], x[2]
+                source = g_words.rearrange("g p n t -> p g (n t)")[:, groups, PACK * N * h : PACK * N * (h + 1)]
+                nc.sync.dma_start(out=g_codes[h][:, groups, :].bitcast(I32), in_=source.bitcast(I32))
             else:
                 c, h = x[1], x[2]
                 source = slope[K * c : K * (c + 1), N * h : N * (h + 1)]
@@ -80,17 +80,21 @@ def tile_augmented_lagrangian_latent_gradient_e3_kernel(
         nc.vector.memset(g_planes[:].rearrange("p g n -> p (g n)").bitcast(U32), 0)
 
         load(("a", 0, 0))
-        load(("a", 0, 1))
+        load(("g", 0, slice(0, 1)))
         for q in range(4):
-            nc.scalar.dma_start(
+            nc.sync.dma_start(
                 out=g_planes[32 * q : 32 * q + 4, :, :].bitcast(I32),
                 in_=g_scales.bitcast(I32)[:, 4 * q : 4 * q + 4, :].rearrange("g r n -> r g n"),
             )
-        nc.scalar.dma_start(out=costs[:], in_=cost.rearrange("(c p t) -> p c t", c=CHUNKS, t=PACK))
+        cost_rows = cost.rearrange("(c p t) -> p c t", c=CHUNKS, t=PACK)
+        nc.sync.dma_start(out=costs[0][:], in_=cost_rows[:, :1])
+        for x in [("a", 0, 1), ("g", 0, slice(1, 2)), ("s", 0, 0), ("a", 1, 0), ("a", 1, 1), ("g", 1, slice(0, 2)),
+                  ("s", 0, 1), ("a", 2, 0)]:
+            load(x)
+        nc.sync.dma_start(out=costs[1][:], in_=cost_rows[:, 1:])
         for x in [
-            ("g", 0), ("s", 0, 0), ("a", 1, 0), ("g", 1), ("s", 0, 1), ("a", 1, 1), ("s", 1, 0),
-            ("a", 2, 0), ("a", 2, 1), ("s", 1, 1), ("w", 0), ("a", 3, 0), ("s", 2, 0), ("a", 3, 1),
-            ("w", 1), ("s", 2, 1), ("w", 2), ("s", 3, 0), ("w", 3), ("s", 3, 1),
+            ("s", 1, 0), ("a", 2, 1), ("w", 0), ("s", 1, 1), ("a", 3, 0), ("a", 3, 1), ("s", 2, 0),
+            ("w", 1), ("s", 2, 1), ("w", 2), ("w", 3), ("s", 3, 0), ("s", 3, 1),
         ]:
             load(x)
         nc.sync.dma_start(out=taus[:], in_=tau.rearrange("(p m) -> p m", m=PACK))
@@ -98,27 +102,41 @@ def tile_augmented_lagrangian_latent_gradient_e3_kernel(
 
         grouped = {}
 
-        def interleave(x, slots, engine):
+        def pool_copy(dst, src):
+            nc.gpsimd.tensor_scalar(out=dst, in0=src, scalar1=1.0, scalar2=0.0, op0=MULT, op1=ADD)
+
+        def pool_buffer_half(i):
+            return stage.tile([P, 2 * K], BF16, name="pool_buffer%d" % (i % 3), align_bytes=64, bufs=1)
+
+        def pool_buffer(i):
+            return stage.tile([P, K * PACK], BF16, name="pool_buffer%d" % (i % 3), align_bytes=64, bufs=1)
+
+        def piece_buffer():
+            return stage.tile([P, 2 * K], BF16, name="piece", align_bytes=64, bufs=6)
+
+        def interleave(x, u, slots, engine):
             source = a_raw[x[1]][x[2]][:] if x[0] == "a" else w_raw[x[1]][:]
-            if x not in grouped:
-                grouped[x] = stage.tile([P, K * PACK], BF16, name="grouped", align_bytes=64, bufs=3)
-            dst = grouped[x][:].rearrange("p (t m i j) -> p t m j i", t=PACK, i=2, j=PACK)[:, slots]
-            src = source.rearrange("p j (m i t) -> p t m j i", i=2, t=PACK)[:, slots]
+            if engine == "gpsimd":
+                pool_copy(
+                    grouped[x, u][:].rearrange("p (t m j) -> p t m j", t=2, j=PACK)[:, slots],
+                    source.rearrange("p j (m t) -> p t m j", t=PACK)[:, 2 * u : 2 * u + 2][:, slots],
+                )
+                return
+            dst = grouped[x, u][:].rearrange("p (t m i j) -> p t m j i", t=2, i=2, j=PACK)[:, slots]
+            src = source.rearrange("p j (m i t) -> p t m j i", i=2, t=PACK)[:, 2 * u : 2 * u + 2][:, slots]
             if engine == "vector":
                 nc.vector.tensor_copy(out=dst, in_=src)
             else:
                 nc.scalar.copy(dst, src)
 
-        def quantise(x, slots):
+        def quantise(x, u):
             if x[0] == "a":
                 codes, planes = a_codes[x[1]][x[2]], a_planes[x[1]][x[2]]
             else:
                 codes, planes = w_codes[x[1]], w_planes[x[1]]
-            columns = slice(P * slots.start, P * slots.stop)
+            columns = slice(2 * P * u, 2 * P * (u + 1))
             nc.vector.quantize_mx(
-                out=codes[:, columns].bitcast(E4M3),
-                scales=planes[:, columns],
-                in_=grouped[x][:, K * slots.start : K * slots.stop],
+                out=codes[:, columns].bitcast(E4M3), scales=planes[:, columns], in_=grouped[x, u][:]
             )
 
         banks = {}
@@ -147,25 +165,29 @@ def tile_augmented_lagrangian_latent_gradient_e3_kernel(
                 nc.vector.scalar_tensor_tensor(
                     out=h_rows[i][:, t, :],
                     in0=banks[i, t][:],
-                    scalar=costs[:, c, t : t + 1],
+                    scalar=costs[0][:, 0, t : t + 1] if c == 0 else costs[1][:, c - 1, t : t + 1],
                     in1=slopes[c, h][:, t, :],
                     op0=ADD,
                     op1=MULT,
                 )
 
-        def interleave_h(i):
-            h_grouped[i] = stage.tile([P, N * PACK], BF16, name="h_grouped", align_bytes=64, bufs=1)
-            dst = h_grouped[i][:].rearrange("p (n i t) -> p n t i", i=4, t=PACK)
-            src = h_rows[i][:].rearrange("p t (n i) -> p n t i", i=4)
-            nc.gpsimd.tensor_scalar(
-                out=h_grouped[i][:].rearrange("p (n t) -> p n t", t=PACK)[:, : 4 * POOL_SHARE],
-                in0=h_rows[i][:].rearrange("p t n -> p n t")[:, : 4 * POOL_SHARE],
-                scalar1=1.0,
-                scalar2=0.0,
-                op0=MULT,
-                op1=ADD,
-            )
-            nc.scalar.copy(dst[:, POOL_SHARE:], src[:, POOL_SHARE:])
+        def interleave_h(i, columns, engine):
+            dst = h_grouped[i][:, PACK * columns.start : PACK * columns.stop]
+            src = h_rows[i][:, :, columns]
+            if engine == "gpsimd":
+                pool_copy(dst.rearrange("p (n t) -> p n t", t=PACK), src.rearrange("p t n -> p n t"))
+                return
+            dst = dst.rearrange("p (n i t) -> p n t i", i=4, t=PACK)
+            src = src.rearrange("p t (n i) -> p n t i", i=4)
+            if engine == "vector":
+                nc.vector.tensor_copy(out=dst, in_=src)
+            else:
+                nc.scalar.copy(dst, src)
+
+        def share_h(i):
+            h_grouped[i] = pool_buffer(i)
+            interleave_h(i, slice(0, POOL_SHARE), "gpsimd")
+            interleave_h(i, slice(POOL_SHARE, N), "scalar")
 
         def quantise_h(i):
             tile = TILES[i]
@@ -200,57 +222,90 @@ def tile_augmented_lagrangian_latent_gradient_e3_kernel(
             )
             nc.sync.dma_start(out=out_rows[:, m, columns], in_=result[:])
 
+        both = slice(0, 2)
+
+        def products(i):
+            pairs = [(t, g) for t in range(PACK) for g in range(GROUPS)]
+            if TILES[i][1] == 0:
+                pairs = [(t, g) for g in range(GROUPS) for t in range(PACK)]
+            for t, g in pairs:
+                first_product(i, t, g)
+
         for g in range(GROUPS):
             x = ("a", 0, g)
-            interleave(x, slice(0, 2), "vector")
-            interleave(x, slice(3, 4), "scalar")
-            interleave(x, slice(2, 3), "vector")
-            quantise(x, slice(0, 2))
-            quantise(x, slice(2, 4))
+            grouped[x, 0], grouped[x, 1] = piece_buffer(), piece_buffer()
+            interleave(x, 0, both, "vector")
+            interleave(x, 1, slice(1, 2), "scalar")
+            interleave(x, 1, slice(0, 1), "vector")
+            quantise(x, 0)
+            quantise(x, 1)
             for t in range(PACK):
                 first_product(0, t, g)
         for m in range(PACK):
             sums[0, m] = psum.tile([P, N], F32, name="sum%d" % m)
 
+        read_banks(0)
+        x, y = ("a", 1, 0), ("a", 1, 1)
+        grouped[x, 0], grouped[x, 1], grouped[y, 0] = piece_buffer(), piece_buffer(), piece_buffer()
+        grouped[y, 1] = pool_buffer_half(0)
+        interleave(x, 0, both, "scalar")
+        interleave(x, 1, both, "gpsimd")
+        interleave(y, 1, both, "scalar")
+        interleave(y, 0, both, "vector")
+        for piece in [(x, 0), (x, 1), (y, 0), (y, 1)]:
+            quantise(*piece)
+        products(1)
+
         last = len(TILES) - 1
-        done = 0
+        pieces = [(x, u) for x in QUEUE for u in range(2)]
         ready = set()
         summed = 0
-        for i in range(last + 1):
+
+        def behind(i):
+            start = sum(PIECES[k] for k in range(1, i))
+            return pieces[start : start + PIECES[i]]
+
+        def scalar_piece(i, k):
+            piece = behind(i)[k]
+            grouped[piece] = pool_buffer_half(i) if k == PIECES[i] - 1 else piece_buffer()
+            interleave(*piece, both, "scalar")
+
+        for i in range(1, last + 1):
             read_banks(i)
-            start, done = done, done + SLOTS[i]
-            for k in range(start // PACK, (done + PACK - 1) // PACK):
-                slots = slice(max(start - PACK * k, 0), min(done - PACK * k, PACK))
-                interleave(QUEUE[k], slots, "scalar")
-                if k == start // PACK and i > 0:
-                    interleave_h(i - 1)
-            for k in range(start // PACK, done // PACK):
-                quantise(QUEUE[k], slice(0, PACK))
-                ready.add(QUEUE[k])
-            if i > 0:
-                quantise_h(i - 1)
-                ready.add(TILES[i - 1])
+            share_h(i - 1)
+            for k in range(AHEAD if i > 1 else 0, PIECES[i]):
+                scalar_piece(i, k)
             if i < last:
-                for g in range(GROUPS):
-                    for t in range(PACK):
-                        first_product(i + 1, t, g)
+                for k in range(AHEAD):
+                    scalar_piece(i + 1, k)
+            for x, u in behind(i):
+                quantise(x, u)
+                if u == 1:
+                    ready.add(x)
+            quantise_h(i - 1)
+            ready.add(TILES[i - 1])
+            if i < last:
+                products(i + 1)
             while summed < CHUNKS - 1 and ("w", summed) in ready and (summed, 0) in ready:
                 for m in range(PACK):
                     second_product(summed, 0, m, summed == 0, False)
                 summed += 1
 
-        interleave_h(last)
+        h_grouped[last] = stage.tile([P, K * PACK], BF16, name="grouped", align_bytes=64, bufs=1)
+        interleave_h(last, slice(0, N // 2), "vector")
+        interleave_h(last, slice(N // 2, N), "scalar")
         for m in range(PACK):
+            if m == 2:
+                for k in range(PACK):
+                    second_product(CHUNKS - 1, 0, k, False, True)
             sums[1, m] = psum.tile([P, N], F32, name="bank%d" % m)
-            second_product(0, 1, m, True, False)
-        for c in range(summed, CHUNKS):
-            for m in range(PACK):
-                second_product(c, 0, m, False, c == CHUNKS - 1)
+            for c in range(CHUNKS - 1):
+                second_product(c, 1, m, c == 0, False)
         for m in range(PACK):
+            if m == 2:
+                quantise_h(last)
             finish(0, m)
-        quantise_h(last)
-        for c in range(1, CHUNKS):
-            for m in range(PACK):
-                second_product(c, 1, m, False, c == CHUNKS - 1)
+        for m in range(PACK):
+            second_product(CHUNKS - 1, 1, m, False, True)
         for m in range(PACK):
             finish(1, m)

@@ -1,6 +1,7 @@
 from contextlib import ExitStack
 
 import concourse.mybir as mybir
+from concourse.masks import make_identity
 
 C, D, L, B = 1024, 2048, 512, 1024
 FLOPS = 2 * C * D * B + 2 * D * L * B
@@ -26,8 +27,8 @@ HALVES = B // N
 TILES = [(c, h) for c in range(CHUNKS) for h in range(HALVES)]
 
 QUEUE = [("a", 2, 0), ("a", 2, 1), ("w", 0), ("a", 3, 0), ("a", 3, 1), ("w", 1), ("w", 2), ("w", 3)]
-PIECES = {1: 1, 2: 3, 3: 2, 4: 3, 5: 2, 6: 3, 7: 2}
-POOL_SHARE = 416
+PIECES = {2: 3, 3: 3, 4: 2, 5: 3, 6: 3, 7: 2}
+POOL_SHARE = 464
 AHEAD = 1
 
 
@@ -55,7 +56,9 @@ def tile_augmented_lagrangian_latent_gradient_e3_kernel(
         w_planes = [sbuf("w_planes%d" % c, [P, L], U8) for c in range(CHUNKS)]
         h_codes = {tile: sbuf("h_codes%d%d" % tile, [P, N], U32) for tile in TILES}
         h_planes = {tile: sbuf("h_planes%d%d" % tile, [P, N], U8) for tile in TILES}
-        costs = [sbuf("costs0", [P, 1, PACK], BF16), sbuf("costs1", [P, CHUNKS - 1, PACK], BF16)]
+        cost_rows = sbuf("cost_rows", [P, K], BF16)
+        costs = sbuf("costs", [P, PACK, CHUNKS], F32)
+        identity = sbuf("identity", [P, P], BF16)
         taus = sbuf("taus", [P, PACK], BF16)
         z_rows = sbuf("z_rows", [P, PACK, B], BF16)
 
@@ -78,22 +81,21 @@ def tile_augmented_lagrangian_latent_gradient_e3_kernel(
                 nc.sync.dma_start(out=slopes[c, h][:], in_=source.rearrange("(p t) n -> p t n", t=PACK))
 
         nc.vector.memset(g_planes[:].rearrange("p g n -> p (g n)").bitcast(U32), 0)
+        nc.vector.memset(cost_rows[:].bitcast(U32), 0)
+        make_identity(nc, identity[:])
 
         load(("a", 0, 0))
+        nc.sync.dma_start(out=cost_rows[:CHUNKS, :], in_=cost.rearrange("(c d) -> c d", c=CHUNKS))
         load(("g", 0, slice(0, 1)))
         for q in range(4):
             nc.sync.dma_start(
                 out=g_planes[32 * q : 32 * q + 4, :, :].bitcast(I32),
                 in_=g_scales.bitcast(I32)[:, 4 * q : 4 * q + 4, :].rearrange("g r n -> r g n"),
             )
-        cost_rows = cost.rearrange("(c p t) -> p c t", c=CHUNKS, t=PACK)
-        nc.sync.dma_start(out=costs[0][:], in_=cost_rows[:, :1])
-        for x in [("a", 0, 1), ("g", 0, slice(1, 2)), ("s", 0, 0), ("a", 1, 0), ("a", 1, 1), ("g", 1, slice(0, 2)),
-                  ("s", 0, 1), ("a", 2, 0)]:
+        for x in [("a", 0, 1), ("g", 0, slice(1, 2)), ("s", 0, 0), ("a", 1, 0), ("g", 1, slice(0, 2)), ("s", 0, 1), ("a", 1, 1)]:
             load(x)
-        nc.sync.dma_start(out=costs[1][:], in_=cost_rows[:, 1:])
         for x in [
-            ("s", 1, 0), ("a", 2, 1), ("w", 0), ("s", 1, 1), ("a", 3, 0), ("a", 3, 1), ("s", 2, 0),
+            ("a", 2, 0), ("s", 1, 0), ("a", 2, 1), ("w", 0), ("s", 1, 1), ("a", 3, 0), ("a", 3, 1), ("s", 2, 0),
             ("w", 1), ("s", 2, 1), ("w", 2), ("w", 3), ("s", 3, 0), ("s", 3, 1),
         ]:
             load(x)
@@ -160,12 +162,13 @@ def tile_augmented_lagrangian_latent_gradient_e3_kernel(
 
         def read_banks(i):
             c, h = TILES[i]
-            h_rows[i] = stage.tile([P, PACK, N], BF16, name="h_rows", align_bytes=64, bufs=2)
+            padded = stage.tile([P, PACK, N + 2], BF16, name="h_rows", align_bytes=64, bufs=2)
+            h_rows[i] = padded[:, :, :N]
             for t in range(PACK):
                 nc.vector.scalar_tensor_tensor(
                     out=h_rows[i][:, t, :],
                     in0=banks[i, t][:],
-                    scalar=costs[0][:, 0, t : t + 1] if c == 0 else costs[1][:, c - 1, t : t + 1],
+                    scalar=costs[:, t, c : c + 1],
                     in1=slopes[c, h][:, t, :],
                     op0=ADD,
                     op1=MULT,
@@ -231,12 +234,18 @@ def tile_augmented_lagrangian_latent_gradient_e3_kernel(
             for t, g in pairs:
                 first_product(i, t, g)
 
+        turned = psum.tile([P, PACK, P], BF16, name="sum0")
+        for t in range(PACK):
+            nc.tensor.transpose(turned[:, t, :], cost_rows[:].rearrange("c (p t) -> c t p", t=PACK)[:, t, :], identity[:])
+
         for g in range(GROUPS):
             x = ("a", 0, g)
             grouped[x, 0], grouped[x, 1] = piece_buffer(), piece_buffer()
             interleave(x, 0, both, "vector")
             interleave(x, 1, slice(1, 2), "scalar")
             interleave(x, 1, slice(0, 1), "vector")
+            if g == 0:
+                nc.scalar.copy(costs[:], turned[:, :, :CHUNKS])
             quantise(x, 0)
             quantise(x, 1)
             for t in range(PACK):
@@ -245,24 +254,34 @@ def tile_augmented_lagrangian_latent_gradient_e3_kernel(
             sums[0, m] = psum.tile([P, N], F32, name="sum%d" % m)
 
         read_banks(0)
-        x, y = ("a", 1, 0), ("a", 1, 1)
-        grouped[x, 0], grouped[x, 1], grouped[y, 0] = piece_buffer(), piece_buffer(), piece_buffer()
-        grouped[y, 1] = pool_buffer_half(0)
+        x = ("a", 1, 0)
+        grouped[x, 0], grouped[x, 1] = pool_buffer_half(0), piece_buffer()
         interleave(x, 0, both, "scalar")
         interleave(x, 1, both, "gpsimd")
-        interleave(y, 1, both, "scalar")
-        interleave(y, 0, both, "vector")
-        for piece in [(x, 0), (x, 1), (y, 0), (y, 1)]:
-            quantise(*piece)
+        quantise(x, 0)
+        quantise(x, 1)
         products(1)
+        read_banks(1)
+        h_grouped[0] = pool_buffer(0)
+        interleave_h(0, slice(0, N // 2), "gpsimd")
+        interleave_h(0, slice(N // 2, N), "scalar")
+        x = ("a", 1, 1)
+        grouped[x, 0], grouped[x, 1] = piece_buffer(), pool_buffer_half(1)
+        interleave(x, 0, both, "scalar")
+        interleave(x, 1, slice(0, 1), "gpsimd")
+        interleave(x, 1, slice(1, 2), "vector")
+        quantise(x, 0)
+        quantise(x, 1)
+        quantise_h(0)
+        products(2)
 
         last = len(TILES) - 1
         pieces = [(x, u) for x in QUEUE for u in range(2)]
-        ready = set()
+        ready = {TILES[0]}
         summed = 0
 
         def behind(i):
-            start = sum(PIECES[k] for k in range(1, i))
+            start = sum(PIECES[k] for k in range(2, i))
             return pieces[start : start + PIECES[i]]
 
         def scalar_piece(i, k):
@@ -270,15 +289,16 @@ def tile_augmented_lagrangian_latent_gradient_e3_kernel(
             grouped[piece] = pool_buffer_half(i) if k == PIECES[i] - 1 else piece_buffer()
             interleave(*piece, both, "scalar")
 
-        for i in range(1, last + 1):
+        scalar_piece(2, 0)
+        for i in range(2, last + 1):
             read_banks(i)
             share_h(i - 1)
-            for k in range(AHEAD if i > 1 else 0, PIECES[i]):
+            for k in range(AHEAD, PIECES[i]):
                 scalar_piece(i, k)
             if i < last:
                 for k in range(AHEAD):
                     scalar_piece(i + 1, k)
-            for x, u in behind(i):
+            for x, u in behind(i)[: 1 if i == last else None]:
                 quantise(x, u)
                 if u == 1:
                     ready.add(x)
@@ -291,8 +311,9 @@ def tile_augmented_lagrangian_latent_gradient_e3_kernel(
                     second_product(summed, 0, m, summed == 0, False)
                 summed += 1
 
-        h_grouped[last] = stage.tile([P, K * PACK], BF16, name="grouped", align_bytes=64, bufs=1)
-        interleave_h(last, slice(0, N // 2), "vector")
+        quantise(*pieces[-1])
+        h_grouped[last] = pool_buffer(last - 1)
+        interleave_h(last, slice(0, N // 2), "gpsimd")
         interleave_h(last, slice(N // 2, N), "scalar")
         for m in range(PACK):
             if m == 2:

@@ -28,8 +28,8 @@ TILES = [(c, h) for c in range(CHUNKS) for h in range(HALVES)]
 
 QUEUE = [("a", 2, 0), ("a", 2, 1), ("w", 0), ("a", 3, 0), ("a", 3, 1), ("w", 1), ("w", 2), ("w", 3)]
 PIECES = {2: 3, 3: 3, 4: 2, 5: 3, 6: 3, 7: 2}
-POOL_SHARE = 464
-AHEAD = 1
+POOL_SHARE = 384
+AHEAD = 2
 
 
 def tile_augmented_lagrangian_latent_gradient_e3_kernel(
@@ -162,8 +162,7 @@ def tile_augmented_lagrangian_latent_gradient_e3_kernel(
 
         def read_banks(i):
             c, h = TILES[i]
-            padded = stage.tile([P, PACK, N + 2], BF16, name="h_rows", align_bytes=64, bufs=2)
-            h_rows[i] = padded[:, :, :N]
+            h_rows[i] = stage.tile([P, PACK, N], BF16, name="h_rows", align_bytes=64, bufs=2)
             for t in range(PACK):
                 nc.vector.scalar_tensor_tensor(
                     out=h_rows[i][:, t, :],
@@ -290,6 +289,7 @@ def tile_augmented_lagrangian_latent_gradient_e3_kernel(
             interleave(*piece, both, "scalar")
 
         scalar_piece(2, 0)
+        scalar_piece(2, 1)
         for i in range(2, last + 1):
             read_banks(i)
             share_h(i - 1)

@@ -27,9 +27,10 @@ HALVES = B // N
 TILES = [(c, h) for c in range(CHUNKS) for h in range(HALVES)]
 
 QUEUE = [("a", 2, 0), ("a", 2, 1), ("w", 0), ("a", 3, 0), ("a", 3, 1), ("w", 1), ("w", 2), ("w", 3)]
-PIECES = {2: 3, 3: 3, 4: 2, 5: 3, 6: 3, 7: 2}
-POOL_SHARE = 384
+PIECES = {2: 3, 3: 3, 4: 2, 5: 3, 6: 2, 7: 3}
+POOL_SHARE = 400
 AHEAD = 2
+LAST_SHARE = 224
 
 
 def tile_augmented_lagrangian_latent_gradient_e3_kernel(
@@ -85,12 +86,12 @@ def tile_augmented_lagrangian_latent_gradient_e3_kernel(
         make_identity(nc, identity[:])
 
         load(("a", 0, 0))
-        nc.sync.dma_start(out=cost_rows[:CHUNKS, :], in_=cost.rearrange("(c d) -> c d", c=CHUNKS))
+        nc.sync.dma_start(out=cost_rows[0 : 4 * CHUNKS : 4, :], in_=cost.rearrange("(c d) -> c d", c=CHUNKS))
         load(("g", 0, slice(0, 1)))
-        for q in range(4):
+        for r in range(4):
             nc.sync.dma_start(
-                out=g_planes[32 * q : 32 * q + 4, :, :].bitcast(I32),
-                in_=g_scales.bitcast(I32)[:, 4 * q : 4 * q + 4, :].rearrange("g r n -> r g n"),
+                out=g_planes[r:P:32, :, :].bitcast(I32),
+                in_=g_scales.bitcast(I32).rearrange("g (q r) n -> r q g n", r=4)[r],
             )
         for x in [("a", 0, 1), ("g", 0, slice(1, 2)), ("s", 0, 0), ("a", 1, 0), ("g", 1, slice(0, 2)), ("s", 0, 1), ("a", 1, 1)]:
             load(x)
@@ -179,8 +180,8 @@ def tile_augmented_lagrangian_latent_gradient_e3_kernel(
             if engine == "gpsimd":
                 pool_copy(dst.rearrange("p (n t) -> p n t", t=PACK), src.rearrange("p t n -> p n t"))
                 return
-            dst = dst.rearrange("p (n i t) -> p n t i", i=4, t=PACK)
-            src = src.rearrange("p t (n i) -> p n t i", i=4)
+            dst = dst.rearrange("p (n i t) -> p n t i", i=2, t=PACK)
+            src = src.rearrange("p t (n i) -> p n t i", i=2)
             if engine == "vector":
                 nc.vector.tensor_copy(out=dst, in_=src)
             else:
@@ -222,7 +223,8 @@ def tile_augmented_lagrangian_latent_gradient_e3_kernel(
                 op0=MULT,
                 op1=ADD,
             )
-            nc.sync.dma_start(out=out_rows[:, m, columns], in_=result[:])
+            queue = nc.sync if m % 2 == 0 else nc.scalar
+            queue.dma_start(out=out_rows[:, m, columns], in_=result[:])
 
         both = slice(0, 2)
 
@@ -244,7 +246,7 @@ def tile_augmented_lagrangian_latent_gradient_e3_kernel(
             interleave(x, 1, slice(1, 2), "scalar")
             interleave(x, 1, slice(0, 1), "vector")
             if g == 0:
-                nc.scalar.copy(costs[:], turned[:, :, :CHUNKS])
+                nc.scalar.copy(costs[:], turned[:, :, 0 : 4 * CHUNKS : 4])
             quantise(x, 0)
             quantise(x, 1)
             for t in range(PACK):
@@ -275,7 +277,8 @@ def tile_augmented_lagrangian_latent_gradient_e3_kernel(
         products(2)
 
         last = len(TILES) - 1
-        pieces = [(x, u) for x in QUEUE for u in range(2)]
+        pieces = [(x, u) for x in QUEUE[:-2] for u in range(2)]
+        pieces += [(x, u) for u in range(2) for x in QUEUE[-2:]]
         ready = {TILES[0]}
         summed = 0
 
@@ -311,17 +314,28 @@ def tile_augmented_lagrangian_latent_gradient_e3_kernel(
                     second_product(summed, 0, m, summed == 0, False)
                 summed += 1
 
-        quantise(*pieces[-1])
+        for piece in pieces[-2:]:
+            quantise(*piece)
         h_grouped[last] = pool_buffer(last - 1)
-        interleave_h(last, slice(0, N // 2), "gpsimd")
-        interleave_h(last, slice(N // 2, N), "scalar")
+        interleave_h(last, slice(0, LAST_SHARE), "gpsimd")
+        interleave_h(last, slice(LAST_SHARE, N), "scalar")
         for m in range(PACK):
-            if m == 2:
-                for k in range(PACK):
-                    second_product(CHUNKS - 1, 0, k, False, True)
             sums[1, m] = psum.tile([P, N], F32, name="bank%d" % m)
-            for c in range(CHUNKS - 1):
+        early, late = range(0, 2), range(2, PACK)
+        for m in early:
+            second_product(CHUNKS - 2, 0, m, False, False)
+        for m in range(PACK):
+            for c in range(CHUNKS - 2):
                 second_product(c, 1, m, c == 0, False)
+        for m in early:
+            second_product(CHUNKS - 1, 0, m, False, True)
+        for m in early:
+            second_product(CHUNKS - 2, 1, m, False, False)
+        for m in late:
+            second_product(CHUNKS - 2, 0, m, False, False)
+            second_product(CHUNKS - 1, 0, m, False, True)
+        for m in late:
+            second_product(CHUNKS - 2, 1, m, False, False)
         for m in range(PACK):
             if m == 2:
                 quantise_h(last)

@@ -25,12 +25,18 @@ CHUNKS = D // K
 HALVES = B // N
 
 TILES = [(c, h) for c in range(CHUNKS) for h in range(HALVES)]
+LAST = len(TILES) - 1
 
-QUEUE = [("a", 2, 0), ("a", 2, 1), ("w", 0), ("a", 3, 0), ("a", 3, 1), ("w", 1), ("w", 2), ("w", 3)]
+EARLY, LATE = range(0, 2), range(2, PACK)
+
+A_PIECES = [[(("a", c, g), u) for g in range(GROUPS) for u in range(2)] for c in range(CHUNKS)]
+W_EARLY = [(("w", c), 0) for c in range(CHUNKS)]
+W_LATE = [(("w", c), 1) for c in range(CHUNKS)]
+QUEUE = A_PIECES[2] + W_EARLY[:2] + A_PIECES[3] + W_EARLY[2:3] + W_LATE[:2] + W_EARLY[3:] + W_LATE[2:]
 PIECES = {2: 3, 3: 3, 4: 2, 5: 3, 6: 2, 7: 3}
-POOL_SHARE = 400
 AHEAD = 2
-LAST_SHARE = 224
+POOL_SHARE = 400
+LAST_SHARE = 160
 
 
 def tile_augmented_lagrangian_latent_gradient_e3_kernel(
@@ -39,7 +45,7 @@ def tile_augmented_lagrangian_latent_gradient_e3_kernel(
     nc = tc.nc
     with ExitStack() as ctx:
         keep = ctx.enter_context(tc.tile_pool(name="keep", bufs=1))
-        stage = ctx.enter_context(tc.tile_pool(name="stage", bufs=3))
+        stage = ctx.enter_context(tc.tile_pool(name="stage", bufs=1))
         psum = ctx.enter_context(tc.psum_pool(name="psum", bufs=1))
         ctx.enter_context(tc.manual_schedule())
 
@@ -48,13 +54,11 @@ def tile_augmented_lagrangian_latent_gradient_e3_kernel(
 
         g_codes = [sbuf("g_codes%d" % h, [P, GROUPS, N], U32) for h in range(HALVES)]
         g_planes = sbuf("g_planes", [P, GROUPS, B], U8)
-        a_raw = [[sbuf("a_raw%d%d" % (c, g), [P, PACK, K], BF16) for g in range(GROUPS)] for c in range(CHUNKS)]
-        a_codes = [[sbuf("a_codes%d%d" % (c, g), [P, K], U32) for g in range(GROUPS)] for c in range(CHUNKS)]
-        a_planes = [[sbuf("a_planes%d%d" % (c, g), [P, K], U8) for g in range(GROUPS)] for c in range(CHUNKS)]
+        operands = [("a", c, g) for c in range(CHUNKS) for g in range(GROUPS)] + [("w", c) for c in range(CHUNKS)]
+        raw = {x: sbuf("raw%d" % n, [P, PACK, K], BF16) for n, x in enumerate(operands)}
+        codes = {x: sbuf("codes%d" % n, [P, K], U32) for n, x in enumerate(operands)}
+        planes = {x: sbuf("planes%d" % n, [P, K], U8) for n, x in enumerate(operands)}
         slopes = {tile: sbuf("slopes%d%d" % tile, [P, PACK, N], BF16) for tile in TILES}
-        w_raw = [sbuf("w_raw%d" % c, [P, PACK, L], BF16) for c in range(CHUNKS)]
-        w_codes = [sbuf("w_codes%d" % c, [P, L], U32) for c in range(CHUNKS)]
-        w_planes = [sbuf("w_planes%d" % c, [P, L], U8) for c in range(CHUNKS)]
         h_codes = {tile: sbuf("h_codes%d%d" % tile, [P, N], U32) for tile in TILES}
         h_planes = {tile: sbuf("h_planes%d%d" % tile, [P, N], U8) for tile in TILES}
         cost_rows = sbuf("cost_rows", [P, K], BF16)
@@ -67,11 +71,10 @@ def tile_augmented_lagrangian_latent_gradient_e3_kernel(
             if x[0] == "a":
                 c, g = x[1], x[2]
                 source = a[K * g : K * (g + 1), K * c : K * (c + 1)]
-                nc.sync.dma_start(out=a_raw[c][g][:], in_=source.rearrange("(p j) d -> p j d", j=PACK))
+                nc.sync.dma_start(out=raw[x][:], in_=source.rearrange("(p j) d -> p j d", j=PACK))
             elif x[0] == "w":
-                c = x[1]
-                source = w[K * c : K * (c + 1), :]
-                nc.sync.dma_start(out=w_raw[c][:], in_=source.rearrange("(p j) l -> p j l", j=PACK))
+                source = w[K * x[1] : K * (x[1] + 1), :]
+                nc.sync.dma_start(out=raw[x][:], in_=source.rearrange("(p j) l -> p j l", j=PACK))
             elif x[0] == "g":
                 h, groups = x[1], x[2]
                 source = g_words.rearrange("g p n t -> p g (n t)")[:, groups, PACK * N * h : PACK * N * (h + 1)]
@@ -86,60 +89,59 @@ def tile_augmented_lagrangian_latent_gradient_e3_kernel(
         make_identity(nc, identity[:])
 
         load(("a", 0, 0))
-        nc.sync.dma_start(out=cost_rows[0 : 4 * CHUNKS : 4, :], in_=cost.rearrange("(c d) -> c d", c=CHUNKS))
+        cost_partitions = slice(0, 4 * CHUNKS, 4)
+        nc.sync.dma_start(out=cost_rows[cost_partitions, :], in_=cost.rearrange("(c d) -> c d", c=CHUNKS))
         load(("g", 0, slice(0, 1)))
         for r in range(4):
             nc.sync.dma_start(
                 out=g_planes[r:P:32, :, :].bitcast(I32),
                 in_=g_scales.bitcast(I32).rearrange("g (q r) n -> r q g n", r=4)[r],
             )
-        for x in [("a", 0, 1), ("g", 0, slice(1, 2)), ("s", 0, 0), ("a", 1, 0), ("g", 1, slice(0, 2)), ("s", 0, 1), ("a", 1, 1)]:
-            load(x)
         for x in [
-            ("a", 2, 0), ("s", 1, 0), ("a", 2, 1), ("w", 0), ("s", 1, 1), ("a", 3, 0), ("a", 3, 1), ("s", 2, 0),
-            ("w", 1), ("s", 2, 1), ("w", 2), ("w", 3), ("s", 3, 0), ("s", 3, 1),
+            ("a", 0, 1), ("g", 0, slice(1, 2)), ("slope", 0, 0),
+            ("a", 1, 0), ("g", 1, slice(0, 2)), ("slope", 0, 1),
+            ("a", 1, 1), ("a", 2, 0), ("slope", 1, 0),
+            ("a", 2, 1), ("w", 0), ("slope", 1, 1),
+            ("w", 1), ("a", 3, 0), ("slope", 2, 0),
+            ("a", 3, 1), ("slope", 2, 1),
+            ("w", 2), ("w", 3), ("slope", 3, 0), ("slope", 3, 1),
         ]:
             load(x)
         nc.sync.dma_start(out=taus[:], in_=tau.rearrange("(p m) -> p m", m=PACK))
         nc.sync.dma_start(out=z_rows[:], in_=z.rearrange("(p m) n -> p m n", m=PACK))
 
-        grouped = {}
+        def piece_buffer():
+            return stage.tile([P, 2 * K], BF16, name="piece", align_bytes=64, bufs=6)
+
+        def gate_buffer(i, width):
+            return stage.tile([P, width], BF16, name="gate%d" % (i % 3), align_bytes=64, bufs=1)
 
         def pool_copy(dst, src):
             nc.gpsimd.tensor_scalar(out=dst, in0=src, scalar1=1.0, scalar2=0.0, op0=MULT, op1=ADD)
 
-        def pool_buffer_half(i):
-            return stage.tile([P, 2 * K], BF16, name="pool_buffer%d" % (i % 3), align_bytes=64, bufs=1)
+        grouped = {}
+        both, first, second = slice(0, 2), slice(0, 1), slice(1, 2)
 
-        def pool_buffer(i):
-            return stage.tile([P, K * PACK], BF16, name="pool_buffer%d" % (i % 3), align_bytes=64, bufs=1)
-
-        def piece_buffer():
-            return stage.tile([P, 2 * K], BF16, name="piece", align_bytes=64, bufs=6)
-
-        def interleave(x, u, slots, engine):
-            source = a_raw[x[1]][x[2]][:] if x[0] == "a" else w_raw[x[1]][:]
+        def interleave(piece, slots, engine):
+            x, u = piece
             if engine == "gpsimd":
                 pool_copy(
-                    grouped[x, u][:].rearrange("p (t m j) -> p t m j", t=2, j=PACK)[:, slots],
-                    source.rearrange("p j (m t) -> p t m j", t=PACK)[:, 2 * u : 2 * u + 2][:, slots],
+                    grouped[piece][:].rearrange("p (t m j) -> p t m j", t=2, j=PACK)[:, slots],
+                    raw[x][:].rearrange("p j (m t) -> p t m j", t=PACK)[:, 2 * u : 2 * u + 2][:, slots],
                 )
                 return
-            dst = grouped[x, u][:].rearrange("p (t m i j) -> p t m j i", t=2, i=2, j=PACK)[:, slots]
-            src = source.rearrange("p j (m i t) -> p t m j i", i=2, t=PACK)[:, 2 * u : 2 * u + 2][:, slots]
+            dst = grouped[piece][:].rearrange("p (t m i j) -> p t m j i", t=2, i=2, j=PACK)[:, slots]
+            src = raw[x][:].rearrange("p j (m i t) -> p t m j i", i=2, t=PACK)[:, 2 * u : 2 * u + 2][:, slots]
             if engine == "vector":
                 nc.vector.tensor_copy(out=dst, in_=src)
             else:
                 nc.scalar.copy(dst, src)
 
-        def quantise(x, u):
-            if x[0] == "a":
-                codes, planes = a_codes[x[1]][x[2]], a_planes[x[1]][x[2]]
-            else:
-                codes, planes = w_codes[x[1]], w_planes[x[1]]
+        def quantise(piece):
+            x, u = piece
             columns = slice(2 * P * u, 2 * P * (u + 1))
             nc.vector.quantize_mx(
-                out=codes[:, columns].bitcast(E4M3), scales=planes[:, columns], in_=grouped[x, u][:]
+                out=codes[x][:, columns].bitcast(E4M3), scales=planes[x][:, columns], in_=grouped[piece][:]
             )
 
         banks = {}
@@ -151,13 +153,20 @@ def tile_augmented_lagrangian_latent_gradient_e3_kernel(
                 banks[i, t] = psum.tile([P, N], F32, name="bank%d" % t)
             nc.tensor.matmul_mx(
                 out=banks[i, t][:],
-                lhsT=a_codes[c][g][:, columns].bitcast(E4M3),
-                lhsT_scale=a_planes[c][g][:, columns],
+                lhsT=codes["a", c, g][:, columns].bitcast(E4M3),
+                lhsT_scale=planes["a", c, g][:, columns],
                 rhs=g_codes[h][:, g, :].bitcast(E5M2),
                 rhs_scale=g_planes[:, g, N * h : N * (h + 1)],
                 start=(g == 0),
                 stop=(g == GROUPS - 1),
             )
+
+        def first_products(i):
+            pairs = [(t, g) for t in range(PACK) for g in range(GROUPS)]
+            if TILES[i][1] == 0:
+                pairs = [(t, g) for g in range(GROUPS) for t in range(PACK)]
+            for t, g in pairs:
+                first_product(i, t, g)
 
         h_rows, h_grouped = {}, {}
 
@@ -174,47 +183,44 @@ def tile_augmented_lagrangian_latent_gradient_e3_kernel(
                     op1=MULT,
                 )
 
-        def interleave_h(i, columns, engine):
-            dst = h_grouped[i][:, PACK * columns.start : PACK * columns.stop]
+        def interleave_h(i, columns, dst, engine):
             src = h_rows[i][:, :, columns]
             if engine == "gpsimd":
                 pool_copy(dst.rearrange("p (n t) -> p n t", t=PACK), src.rearrange("p t n -> p n t"))
-                return
-            dst = dst.rearrange("p (n i t) -> p n t i", i=2, t=PACK)
-            src = src.rearrange("p t (n i) -> p n t i", i=2)
-            if engine == "vector":
-                nc.vector.tensor_copy(out=dst, in_=src)
             else:
-                nc.scalar.copy(dst, src)
+                nc.scalar.copy(
+                    dst.rearrange("p (n i t) -> p n t i", i=4, t=PACK), src.rearrange("p t (n i) -> p n t i", i=4)
+                )
 
-        def share_h(i):
-            h_grouped[i] = pool_buffer(i)
-            interleave_h(i, slice(0, POOL_SHARE), "gpsimd")
-            interleave_h(i, slice(POOL_SHARE, N), "scalar")
+        def share_h(i, share):
+            h_grouped[i] = gate_buffer(i, PACK * N)
+            interleave_h(i, slice(0, share), h_grouped[i][:, : PACK * share], "gpsimd")
+            interleave_h(i, slice(share, N), h_grouped[i][:, PACK * share :], "scalar")
 
-        def quantise_h(i):
-            tile = TILES[i]
-            nc.vector.quantize_mx(out=h_codes[tile][:].bitcast(E5M2), scales=h_planes[tile][:], in_=h_grouped[i][:])
+        def quantise_h(i, columns, source):
+            nc.vector.quantize_mx(
+                out=h_codes[TILES[i]][:, columns].bitcast(E5M2), scales=h_planes[TILES[i]][:, columns], in_=source
+            )
 
         sums = {}
 
-        def second_product(c, h, m, start, stop):
+        def second_product(c, h, m):
             columns = slice(P * m, P * (m + 1))
             nc.tensor.matmul_mx(
                 out=sums[h, m][:],
-                lhsT=w_codes[c][:, columns].bitcast(E4M3),
-                lhsT_scale=w_planes[c][:, columns],
+                lhsT=codes["w", c][:, columns].bitcast(E4M3),
+                lhsT_scale=planes["w", c][:, columns],
                 rhs=h_codes[c, h][:].bitcast(E5M2),
                 rhs_scale=h_planes[c, h][:],
-                start=start,
-                stop=stop,
+                start=(c == 0),
+                stop=(c == CHUNKS - 1),
             )
 
         out_rows = out.rearrange("(p m) n -> p m n", m=PACK)
 
         def finish(h, m):
             columns = slice(N * h, N * (h + 1))
-            result = stage.tile([P, N], F32, name="result", align_bytes=64, bufs=8)
+            result = stage.tile([P, N], F32, name="result", align_bytes=64, bufs=HALVES * PACK)
             nc.vector.scalar_tensor_tensor(
                 out=result[:],
                 in0=z_rows[:, m, columns],
@@ -226,121 +232,104 @@ def tile_augmented_lagrangian_latent_gradient_e3_kernel(
             queue = nc.sync if m % 2 == 0 else nc.scalar
             queue.dma_start(out=out_rows[:, m, columns], in_=result[:])
 
-        both = slice(0, 2)
-
-        def products(i):
-            pairs = [(t, g) for t in range(PACK) for g in range(GROUPS)]
-            if TILES[i][1] == 0:
-                pairs = [(t, g) for g in range(GROUPS) for t in range(PACK)]
-            for t, g in pairs:
-                first_product(i, t, g)
-
         turned = psum.tile([P, PACK, P], BF16, name="sum0")
         for t in range(PACK):
             nc.tensor.transpose(turned[:, t, :], cost_rows[:].rearrange("c (p t) -> c t p", t=PACK)[:, t, :], identity[:])
 
         for g in range(GROUPS):
-            x = ("a", 0, g)
-            grouped[x, 0], grouped[x, 1] = piece_buffer(), piece_buffer()
-            interleave(x, 0, both, "vector")
-            interleave(x, 1, slice(1, 2), "scalar")
-            interleave(x, 1, slice(0, 1), "vector")
+            low, high = A_PIECES[0][2 * g : 2 * g + 2]
+            grouped[low], grouped[high] = piece_buffer(), piece_buffer()
+            interleave(low, both, "vector")
+            interleave(high, second, "scalar")
+            interleave(high, first, "vector")
             if g == 0:
-                nc.scalar.copy(costs[:], turned[:, :, 0 : 4 * CHUNKS : 4])
-            quantise(x, 0)
-            quantise(x, 1)
+                nc.scalar.copy(costs[:], turned[:, :, cost_partitions])
+            quantise(low)
+            quantise(high)
             for t in range(PACK):
                 first_product(0, t, g)
-        for m in range(PACK):
-            sums[0, m] = psum.tile([P, N], F32, name="sum%d" % m)
+        for h in range(HALVES):
+            for m in EARLY:
+                sums[h, m] = psum.tile([P, N], F32, name="sum%d" % (2 * h + m))
 
         read_banks(0)
-        x = ("a", 1, 0)
-        grouped[x, 0], grouped[x, 1] = pool_buffer_half(0), piece_buffer()
-        interleave(x, 0, both, "scalar")
-        interleave(x, 1, both, "gpsimd")
-        quantise(x, 0)
-        quantise(x, 1)
-        products(1)
+        low, high = A_PIECES[1][:2]
+        grouped[low], grouped[high] = gate_buffer(0, 2 * K), piece_buffer()
+        interleave(low, both, "scalar")
+        interleave(high, both, "gpsimd")
+        quantise(low)
+        quantise(high)
+        first_products(1)
         read_banks(1)
-        h_grouped[0] = pool_buffer(0)
-        interleave_h(0, slice(0, N // 2), "gpsimd")
-        interleave_h(0, slice(N // 2, N), "scalar")
-        x = ("a", 1, 1)
-        grouped[x, 0], grouped[x, 1] = piece_buffer(), pool_buffer_half(1)
-        interleave(x, 0, both, "scalar")
-        interleave(x, 1, slice(0, 1), "gpsimd")
-        interleave(x, 1, slice(1, 2), "vector")
-        quantise(x, 0)
-        quantise(x, 1)
-        quantise_h(0)
-        products(2)
-
-        last = len(TILES) - 1
-        pieces = [(x, u) for x in QUEUE[:-2] for u in range(2)]
-        pieces += [(x, u) for u in range(2) for x in QUEUE[-2:]]
-        ready = {TILES[0]}
-        summed = 0
+        share_h(0, N // 2)
+        low, high = A_PIECES[1][2:]
+        grouped[low], grouped[high] = piece_buffer(), gate_buffer(1, 2 * K)
+        interleave(low, both, "scalar")
+        interleave(high, first, "gpsimd")
+        interleave(high, second, "vector")
+        quantise(low)
+        quantise(high)
+        quantise_h(0, slice(0, N), h_grouped[0][:])
+        first_products(2)
 
         def behind(i):
             start = sum(PIECES[k] for k in range(2, i))
-            return pieces[start : start + PIECES[i]]
+            return QUEUE[start : start + PIECES[i]]
 
-        def scalar_piece(i, k):
-            piece = behind(i)[k]
-            grouped[piece] = pool_buffer_half(i) if k == PIECES[i] - 1 else piece_buffer()
-            interleave(*piece, both, "scalar")
+        def scalar_pieces(i, which):
+            for piece in behind(i)[which]:
+                grouped[piece] = gate_buffer(i, 2 * K) if piece == behind(i)[-1] else piece_buffer()
+                interleave(piece, both, "scalar")
 
-        scalar_piece(2, 0)
-        scalar_piece(2, 1)
-        for i in range(2, last + 1):
+        ready = {TILES[0]}
+        summed = []
+        scalar_pieces(2, slice(0, AHEAD))
+        for i in range(2, LAST + 1):
             read_banks(i)
-            share_h(i - 1)
-            for k in range(AHEAD, PIECES[i]):
-                scalar_piece(i, k)
-            if i < last:
-                for k in range(AHEAD):
-                    scalar_piece(i + 1, k)
-            for x, u in behind(i)[: 1 if i == last else None]:
-                quantise(x, u)
-                if u == 1:
-                    ready.add(x)
-            quantise_h(i - 1)
+            share_h(i - 1, POOL_SHARE)
+            scalar_pieces(i, slice(AHEAD, None))
+            if i < LAST:
+                scalar_pieces(i + 1, slice(0, AHEAD))
+            for piece in behind(i)[: 1 if i == LAST else None]:
+                quantise(piece)
+                ready.add(piece)
+            quantise_h(i - 1, slice(0, N), h_grouped[i - 1][:])
             ready.add(TILES[i - 1])
-            if i < last:
-                products(i + 1)
-            while summed < CHUNKS - 1 and ("w", summed) in ready and (summed, 0) in ready:
-                for m in range(PACK):
-                    second_product(summed, 0, m, summed == 0, False)
-                summed += 1
+            if i < LAST:
+                first_products(i + 1)
+            for c, h in TILES[: LAST - 1]:
+                if (c, h) not in summed and (c, h) in ready and W_EARLY[c] in ready:
+                    for m in EARLY:
+                        second_product(c, h, m)
+                    summed.append((c, h))
 
-        for piece in pieces[-2:]:
-            quantise(*piece)
-        h_grouped[last] = pool_buffer(last - 1)
-        interleave_h(last, slice(0, LAST_SHARE), "gpsimd")
-        interleave_h(last, slice(LAST_SHARE, N), "scalar")
-        for m in range(PACK):
-            sums[1, m] = psum.tile([P, N], F32, name="bank%d" % m)
-        early, late = range(0, 2), range(2, PACK)
-        for m in early:
-            second_product(CHUNKS - 2, 0, m, False, False)
-        for m in range(PACK):
-            for c in range(CHUNKS - 2):
-                second_product(c, 1, m, c == 0, False)
-        for m in early:
-            second_product(CHUNKS - 1, 0, m, False, True)
-        for m in early:
-            second_product(CHUNKS - 2, 1, m, False, False)
-        for m in late:
-            second_product(CHUNKS - 2, 0, m, False, False)
-            second_product(CHUNKS - 1, 0, m, False, True)
-        for m in late:
-            second_product(CHUNKS - 2, 1, m, False, False)
-        for m in range(PACK):
-            if m == 2:
-                quantise_h(last)
+        for piece in W_LATE[2:]:
+            quantise(piece)
+        middle = N // 2
+        cut = middle + LAST_SHARE
+        parts = [piece_buffer(), gate_buffer(LAST - 1, 2 * K)]
+        interleave_h(LAST, slice(0, middle), parts[0][:], "scalar")
+        interleave_h(LAST, slice(middle, cut), parts[1][:, : PACK * LAST_SHARE], "gpsimd")
+        interleave_h(LAST, slice(cut, N), parts[1][:, PACK * LAST_SHARE :], "scalar")
+        for h in range(HALVES):
+            for m in LATE:
+                sums[h, m] = psum.tile([P, N], F32, name="bank%d" % (2 * h + m - 2))
+                for c in range(CHUNKS - 2):
+                    second_product(c, h, m)
+        for m in EARLY:
+            second_product(CHUNKS - 1, 0, m)
+        for m in LATE:
+            second_product(CHUNKS - 2, 0, m)
+            second_product(CHUNKS - 1, 0, m)
+        for m in LATE:
+            second_product(CHUNKS - 2, 1, m)
+        for m in EARLY:
+            finish(0, m)
+        quantise_h(LAST, slice(0, middle), parts[0][:])
+        quantise_h(LAST, slice(middle, N), parts[1][:])
+        for m in LATE:
             finish(0, m)
         for m in range(PACK):
-            second_product(CHUNKS - 1, 1, m, False, True)
+            second_product(CHUNKS - 1, 1, m)
         for m in range(PACK):
             finish(1, m)

@@ -33,9 +33,9 @@ A_PIECES = [[(("a", c, g), u) for g in range(GROUPS) for u in range(2)] for c in
 W_EARLY = [(("w", c), 0) for c in range(CHUNKS)]
 W_LATE = [(("w", c), 1) for c in range(CHUNKS)]
 QUEUE = A_PIECES[2] + W_EARLY[:2] + A_PIECES[3] + W_EARLY[2:3] + W_LATE[:2] + W_EARLY[3:] + W_LATE[2:]
-PIECES = {2: 3, 3: 3, 4: 2, 5: 3, 6: 2, 7: 3}
+CALLS = {2: (2, 1), 3: (1, 2), 4: (2,), 5: (2, 1), 6: (2,), 7: (1, 2)}
 AHEAD = 2
-POOL_SHARE = 400
+POOL_SHARE = 448
 LAST_SHARE = 160
 
 
@@ -56,8 +56,17 @@ def tile_augmented_lagrangian_latent_gradient_e3_kernel(
         g_planes = sbuf("g_planes", [P, GROUPS, B], U8)
         operands = [("a", c, g) for c in range(CHUNKS) for g in range(GROUPS)] + [("w", c) for c in range(CHUNKS)]
         raw = {x: sbuf("raw%d" % n, [P, PACK, K], BF16) for n, x in enumerate(operands)}
-        codes = {x: sbuf("codes%d" % n, [P, K], U32) for n, x in enumerate(operands)}
-        planes = {x: sbuf("planes%d" % n, [P, K], U8) for n, x in enumerate(operands)}
+        a_operands = operands[: CHUNKS * GROUPS]
+        a_codes = {x: sbuf("codes%d" % n, [P, K], U32) for n, x in enumerate(a_operands)}
+        a_planes = {x: sbuf("planes%d" % n, [P, K], U8) for n, x in enumerate(a_operands)}
+        w_codes = sbuf("w_codes", [P, CHUNKS * L], U32)
+        w_planes = sbuf("w_planes", [P, CHUNKS * L], U8)
+
+        def place(piece):
+            x, u = piece
+            if x[0] == "a":
+                return a_codes[x], a_planes[x], 2 * P * u
+            return w_codes, w_planes, 2 * P * (W_EARLY + W_LATE).index(piece)
         slopes = {tile: sbuf("slopes%d%d" % tile, [P, PACK, N], BF16) for tile in TILES}
         h_codes = {tile: sbuf("h_codes%d%d" % tile, [P, N], U32) for tile in TILES}
         h_planes = {tile: sbuf("h_planes%d%d" % tile, [P, N], U8) for tile in TILES}
@@ -110,8 +119,8 @@ def tile_augmented_lagrangian_latent_gradient_e3_kernel(
         nc.sync.dma_start(out=taus[:], in_=tau.rearrange("(p m) -> p m", m=PACK))
         nc.sync.dma_start(out=z_rows[:], in_=z.rearrange("(p m) n -> p m n", m=PACK))
 
-        def piece_buffer():
-            return stage.tile([P, 2 * K], BF16, name="piece", align_bytes=64, bufs=6)
+        def piece_buffer(count):
+            return stage.tile([P, 2 * K * count], BF16, name="piece", align_bytes=64, bufs=4)
 
         def gate_buffer(i, width):
             return stage.tile([P, width], BF16, name="gate%d" % (i % 3), align_bytes=64, bufs=1)
@@ -126,23 +135,21 @@ def tile_augmented_lagrangian_latent_gradient_e3_kernel(
             x, u = piece
             if engine == "gpsimd":
                 pool_copy(
-                    grouped[piece][:].rearrange("p (t m j) -> p t m j", t=2, j=PACK)[:, slots],
+                    grouped[piece].rearrange("p (t m j) -> p t m j", t=2, j=PACK)[:, slots],
                     raw[x][:].rearrange("p j (m t) -> p t m j", t=PACK)[:, 2 * u : 2 * u + 2][:, slots],
                 )
                 return
-            dst = grouped[piece][:].rearrange("p (t m i j) -> p t m j i", t=2, i=2, j=PACK)[:, slots]
+            dst = grouped[piece].rearrange("p (t m i j) -> p t m j i", t=2, i=2, j=PACK)[:, slots]
             src = raw[x][:].rearrange("p j (m i t) -> p t m j i", i=2, t=PACK)[:, 2 * u : 2 * u + 2][:, slots]
             if engine == "vector":
                 nc.vector.tensor_copy(out=dst, in_=src)
             else:
                 nc.scalar.copy(dst, src)
 
-        def quantise(piece):
-            x, u = piece
-            columns = slice(2 * P * u, 2 * P * (u + 1))
-            nc.vector.quantize_mx(
-                out=codes[x][:, columns].bitcast(E4M3), scales=planes[x][:, columns], in_=grouped[piece][:]
-            )
+        def quantise(call, source):
+            codes, planes, start = place(call[0])
+            columns = slice(start, start + 2 * P * len(call))
+            nc.vector.quantize_mx(out=codes[:, columns].bitcast(E4M3), scales=planes[:, columns], in_=source)
 
         banks = {}
 
@@ -153,8 +160,8 @@ def tile_augmented_lagrangian_latent_gradient_e3_kernel(
                 banks[i, t] = psum.tile([P, N], F32, name="bank%d" % t)
             nc.tensor.matmul_mx(
                 out=banks[i, t][:],
-                lhsT=codes["a", c, g][:, columns].bitcast(E4M3),
-                lhsT_scale=planes["a", c, g][:, columns],
+                lhsT=a_codes["a", c, g][:, columns].bitcast(E4M3),
+                lhsT_scale=a_planes["a", c, g][:, columns],
                 rhs=g_codes[h][:, g, :].bitcast(E5M2),
                 rhs_scale=g_planes[:, g, N * h : N * (h + 1)],
                 start=(g == 0),
@@ -186,7 +193,9 @@ def tile_augmented_lagrangian_latent_gradient_e3_kernel(
         def interleave_h(i, columns, dst, engine):
             src = h_rows[i][:, :, columns]
             if engine == "gpsimd":
-                pool_copy(dst.rearrange("p (n t) -> p n t", t=PACK), src.rearrange("p t n -> p n t"))
+                pool_copy(
+                    dst.rearrange("p (n i t) -> p n t i", i=4, t=PACK), src.rearrange("p t (n i) -> p n t i", i=4)
+                )
             else:
                 nc.scalar.copy(
                     dst.rearrange("p (n i t) -> p n t i", i=4, t=PACK), src.rearrange("p t (n i) -> p n t i", i=4)
@@ -205,11 +214,12 @@ def tile_augmented_lagrangian_latent_gradient_e3_kernel(
         sums = {}
 
         def second_product(c, h, m):
-            columns = slice(P * m, P * (m + 1))
+            start = place((("w", c), m // 2))[2] + P * (m % 2)
+            columns = slice(start, start + P)
             nc.tensor.matmul_mx(
                 out=sums[h, m][:],
-                lhsT=codes["w", c][:, columns].bitcast(E4M3),
-                lhsT_scale=planes["w", c][:, columns],
+                lhsT=w_codes[:, columns].bitcast(E4M3),
+                lhsT_scale=w_planes[:, columns],
                 rhs=h_codes[c, h][:].bitcast(E5M2),
                 rhs_scale=h_planes[c, h][:],
                 start=(c == 0),
@@ -238,14 +248,14 @@ def tile_augmented_lagrangian_latent_gradient_e3_kernel(
 
         for g in range(GROUPS):
             low, high = A_PIECES[0][2 * g : 2 * g + 2]
-            grouped[low], grouped[high] = piece_buffer(), piece_buffer()
+            grouped[low], grouped[high] = piece_buffer(1)[:], piece_buffer(1)[:]
             interleave(low, both, "vector")
             interleave(high, second, "scalar")
             interleave(high, first, "vector")
             if g == 0:
                 nc.scalar.copy(costs[:], turned[:, :, cost_partitions])
-            quantise(low)
-            quantise(high)
+            quantise([low], grouped[low])
+            quantise([high], grouped[high])
             for t in range(PACK):
                 first_product(0, t, g)
         for h in range(HALVES):
@@ -254,31 +264,40 @@ def tile_augmented_lagrangian_latent_gradient_e3_kernel(
 
         read_banks(0)
         low, high = A_PIECES[1][:2]
-        grouped[low], grouped[high] = gate_buffer(0, 2 * K), piece_buffer()
+        grouped[low], grouped[high] = gate_buffer(0, 2 * K)[:], piece_buffer(1)[:]
         interleave(low, both, "scalar")
         interleave(high, both, "gpsimd")
-        quantise(low)
-        quantise(high)
+        quantise([low], grouped[low])
+        quantise([high], grouped[high])
         first_products(1)
         read_banks(1)
         share_h(0, N // 2)
         low, high = A_PIECES[1][2:]
-        grouped[low], grouped[high] = piece_buffer(), gate_buffer(1, 2 * K)
+        grouped[low], grouped[high] = piece_buffer(1)[:], gate_buffer(1, 2 * K)[:]
         interleave(low, both, "scalar")
         interleave(high, first, "gpsimd")
         interleave(high, second, "vector")
-        quantise(low)
-        quantise(high)
+        quantise([low], grouped[low])
+        quantise([high], grouped[high])
         quantise_h(0, slice(0, N), h_grouped[0][:])
         first_products(2)
 
-        def behind(i):
-            start = sum(PIECES[k] for k in range(2, i))
-            return QUEUE[start : start + PIECES[i]]
+        calls, buffers = {}, {}
+        start = 0
+        for i in range(2, LAST + 1):
+            calls[i] = []
+            for count in CALLS[i]:
+                calls[i].append(tuple(QUEUE[start : start + count]))
+                start += count
 
         def scalar_pieces(i, which):
-            for piece in behind(i)[which]:
-                grouped[piece] = gate_buffer(i, 2 * K) if piece == behind(i)[-1] else piece_buffer()
+            for piece in [piece for call in calls[i] for piece in call][which]:
+                call = [call for call in calls[i] if piece in call][0]
+                if piece == call[0]:
+                    gate = call == calls[i][-1] and i < LAST
+                    buffers[call] = gate_buffer(i, 2 * K * len(call)) if gate else piece_buffer(len(call))
+                k = call.index(piece)
+                grouped[piece] = buffers[call][:, 2 * K * k : 2 * K * (k + 1)]
                 interleave(piece, both, "scalar")
 
         ready = {TILES[0]}
@@ -290,9 +309,10 @@ def tile_augmented_lagrangian_latent_gradient_e3_kernel(
             scalar_pieces(i, slice(AHEAD, None))
             if i < LAST:
                 scalar_pieces(i + 1, slice(0, AHEAD))
-            for piece in behind(i)[: 1 if i == LAST else None]:
-                quantise(piece)
-                ready.add(piece)
+            for call in calls[i][: 1 if i == LAST else None]:
+                quantise(call, buffers[call][:])
+                for piece in call:
+                    ready.add(piece)
             quantise_h(i - 1, slice(0, N), h_grouped[i - 1][:])
             ready.add(TILES[i - 1])
             if i < LAST:
@@ -303,11 +323,10 @@ def tile_augmented_lagrangian_latent_gradient_e3_kernel(
                         second_product(c, h, m)
                     summed.append((c, h))
 
-        for piece in W_LATE[2:]:
-            quantise(piece)
+        quantise(calls[LAST][-1], buffers[calls[LAST][-1]][:])
         middle = N // 2
         cut = middle + LAST_SHARE
-        parts = [piece_buffer(), gate_buffer(LAST - 1, 2 * K)]
+        parts = [piece_buffer(1), gate_buffer(LAST - 1, 2 * K)]
         interleave_h(LAST, slice(0, middle), parts[0][:], "scalar")
         interleave_h(LAST, slice(middle, cut), parts[1][:, : PACK * LAST_SHARE], "gpsimd")
         interleave_h(LAST, slice(cut, N), parts[1][:, PACK * LAST_SHARE :], "scalar")

@@ -71,7 +71,7 @@ def tile_augmented_lagrangian_latent_gradient_e3_kernel(
         h_codes = {tile: sbuf("h_codes%d%d" % tile, [P, N], U32) for tile in TILES}
         h_planes = {tile: sbuf("h_planes%d%d" % tile, [P, N], U8) for tile in TILES}
         cost_rows = sbuf("cost_rows", [P, K], BF16)
-        costs = sbuf("costs", [P, PACK, CHUNKS], F32)
+        costs = sbuf("costs", [P, PACK, CHUNKS], BF16)
         identity = sbuf("identity", [P, P], BF16)
         taus = sbuf("taus", [P, PACK], BF16)
         z_rows = sbuf("z_rows", [P, PACK, B], BF16)
@@ -239,8 +239,7 @@ def tile_augmented_lagrangian_latent_gradient_e3_kernel(
                 op0=MULT,
                 op1=ADD,
             )
-            queue = nc.sync if m % 2 == 0 else nc.scalar
-            queue.dma_start(out=out_rows[:, m, columns], in_=result[:])
+            nc.sync.dma_start(out=out_rows[:, m, columns], in_=result[:])
 
         turned = psum.tile([P, PACK, P], BF16, name="sum0")
         for t in range(PACK):

@@ -32,8 +32,8 @@ EARLY, LATE = range(0, 2), range(2, PACK)
 A_PIECES = [[(("a", c, g), u) for g in range(GROUPS) for u in range(2)] for c in range(CHUNKS)]
 W_EARLY = [(("w", c), 0) for c in range(CHUNKS)]
 W_LATE = [(("w", c), 1) for c in range(CHUNKS)]
-QUEUE = A_PIECES[2] + W_EARLY[:2] + A_PIECES[3] + W_EARLY[2:3] + W_LATE[:2] + W_EARLY[3:] + W_LATE[2:]
-CALLS = {2: (2, 1), 3: (1, 2), 4: (2,), 5: (2, 1), 6: (2,), 7: (1, 2)}
+QUEUE = A_PIECES[2] + W_EARLY[:1] + A_PIECES[3][:2] + W_EARLY[1:2] + A_PIECES[3][2:] + W_EARLY[2:3] + W_LATE[:2] + W_EARLY[3:] + W_LATE[2:]
+CALLS = {2: (2, 1), 3: (1, 1), 4: (2, 1), 5: (2, 1), 6: (2,), 7: (1, 2)}
 AHEAD = 2
 POOL_SHARE = 448
 LAST_SHARE = 160
@@ -110,9 +110,9 @@ def tile_augmented_lagrangian_latent_gradient_e3_kernel(
             ("a", 0, 1), ("g", 0, slice(1, 2)), ("slope", 0, 0),
             ("a", 1, 0), ("g", 1, slice(0, 2)), ("slope", 0, 1),
             ("a", 1, 1), ("a", 2, 0), ("slope", 1, 0),
-            ("a", 2, 1), ("w", 0), ("slope", 1, 1),
-            ("w", 1), ("a", 3, 0), ("slope", 2, 0),
-            ("a", 3, 1), ("slope", 2, 1),
+            ("a", 2, 1), ("slope", 1, 1),
+            ("w", 0), ("a", 3, 0), ("slope", 2, 0),
+            ("w", 1), ("a", 3, 1), ("slope", 2, 1),
             ("w", 2), ("w", 3), ("slope", 3, 0), ("slope", 3, 1),
         ]:
             load(x)

@@ -24,17 +24,19 @@ GROUPS = C // K
 CHUNKS = D // K
 HALVES = B // N
 
-TILES = [(c, h) for c in range(CHUNKS) for h in range(HALVES)]
+TILES = [(0, 0), (1, 0), (0, 1), (1, 1), (2, 0), (2, 1), (3, 0), (3, 1)]
 LAST = len(TILES) - 1
+WHOLE_FROM = 0
 
 EARLY, LATE = range(0, 2), range(2, PACK)
 
 A_PIECES = [[(("a", c, g), u) for g in range(GROUPS) for u in range(2)] for c in range(CHUNKS)]
+BY_SLOTS = [(("a", 2, g), u) for u in range(2) for g in range(GROUPS)]
 W_EARLY = [(("w", c), 0) for c in range(CHUNKS)]
 W_LATE = [(("w", c), 1) for c in range(CHUNKS)]
-QUEUE = A_PIECES[2] + W_EARLY[:1] + A_PIECES[3][:2] + W_EARLY[1:2] + A_PIECES[3][2:] + W_EARLY[2:3] + W_LATE[:2] + W_EARLY[3:] + W_LATE[2:]
-CALLS = {2: (2, 1), 3: (1, 1), 4: (2, 1), 5: (2, 1), 6: (2,), 7: (1, 2)}
-AHEAD = 2
+QUEUE = BY_SLOTS + A_PIECES[3][:2] + W_EARLY[:1] + A_PIECES[3][2:] + W_EARLY[1:2] + W_LATE[:2] + W_EARLY[2:] + W_LATE[2:]
+CALLS = {2: (1,), 3: (1, 1, 1), 4: (2, 1), 5: (2, 1), 6: (2, 1), 7: (1, 2)}
+AHEAD = 1
 POOL_SHARE = 448
 LAST_SHARE = 160
 
@@ -53,9 +55,13 @@ def tile_augmented_lagrangian_latent_gradient_e3_kernel(
             return keep.tile(shape, dtype, name=name, align_bytes=64)
 
         g_codes = [sbuf("g_codes%d" % h, [P, GROUPS, N], U32) for h in range(HALVES)]
-        g_planes = sbuf("g_planes", [P, GROUPS, B], U8)
+        g_planes = [sbuf("g_planes%d" % h, [P, GROUPS, N], U8) for h in range(HALVES)]
         operands = [("a", c, g) for c in range(CHUNKS) for g in range(GROUPS)] + [("w", c) for c in range(CHUNKS)]
-        raw = {x: sbuf("raw%d" % n, [P, PACK, K], BF16) for n, x in enumerate(operands)}
+        wide = [sbuf("wide%d" % g, [P, PACK, 2 * K], BF16) for g in range(GROUPS)]
+        raw = {("a", c, g): wide[g][:, :, K * c : K * (c + 1)] for c in range(2) for g in range(GROUPS)}
+        for n, x in enumerate(operands):
+            if x not in raw:
+                raw[x] = sbuf("raw%d" % n, [P, PACK, K], BF16)
         a_operands = operands[: CHUNKS * GROUPS]
         a_codes = {x: sbuf("codes%d" % n, [P, K], U32) for n, x in enumerate(a_operands)}
         a_planes = {x: sbuf("planes%d" % n, [P, K], U8) for n, x in enumerate(a_operands)}
@@ -67,7 +73,17 @@ def tile_augmented_lagrangian_latent_gradient_e3_kernel(
             if x[0] == "a":
                 return a_codes[x], a_planes[x], 2 * P * u
             return w_codes, w_planes, 2 * P * (W_EARLY + W_LATE).index(piece)
-        slopes = {tile: sbuf("slopes%d%d" % tile, [P, PACK, N], BF16) for tile in TILES}
+        slopes = {}
+        for c in range(CHUNKS):
+            for u in range(2):
+                for h in range(HALVES) if c < WHOLE_FROM else [None]:
+                    slopes[c, h, u] = sbuf("slopes%d%s%d" % (c, h, u), [P, 2, B if h is None else N], BF16)
+
+        def slope_row(c, h, t):
+            if c < WHOLE_FROM:
+                return slopes[c, h, t // 2][:, t % 2, :]
+            return slopes[c, None, t // 2][:, t % 2, N * h : N * (h + 1)]
+
         h_codes = {tile: sbuf("h_codes%d%d" % tile, [P, N], U32) for tile in TILES}
         h_planes = {tile: sbuf("h_planes%d%d" % tile, [P, N], U8) for tile in TILES}
         cost_rows = sbuf("cost_rows", [P, K], BF16)
@@ -77,7 +93,10 @@ def tile_augmented_lagrangian_latent_gradient_e3_kernel(
         z_rows = sbuf("z_rows", [P, PACK, B], BF16)
 
         def load(x):
-            if x[0] == "a":
+            if x[0] == "wide":
+                source = a[K * x[1] : K * (x[1] + 1), : 2 * K]
+                nc.sync.dma_start(out=wide[x[1]][:], in_=source.rearrange("(p j) d -> p j d", j=PACK))
+            elif x[0] == "a":
                 c, g = x[1], x[2]
                 source = a[K * g : K * (g + 1), K * c : K * (c + 1)]
                 nc.sync.dma_start(out=raw[x][:], in_=source.rearrange("(p j) d -> p j d", j=PACK))
@@ -88,32 +107,28 @@ def tile_augmented_lagrangian_latent_gradient_e3_kernel(
                 h, groups = x[1], x[2]
                 source = g_words.rearrange("g p n t -> p g (n t)")[:, groups, PACK * N * h : PACK * N * (h + 1)]
                 nc.sync.dma_start(out=g_codes[h][:, groups, :].bitcast(I32), in_=source.bitcast(I32))
+            elif x[0] == "planes":
+                h = x[1]
+                rows = g_scales[:, :, N * h : N * (h + 1)].bitcast(I32).rearrange("g (q r) n -> r q g n", r=4)
+                for r in range(4):
+                    nc.sync.dma_start(out=g_planes[h][r:P:32, :, :].bitcast(I32), in_=rows[r])
+            elif x[0] == "cost":
+                nc.sync.dma_start(out=cost_rows[cost_partitions, :], in_=cost.rearrange("(c d) -> c d", c=CHUNKS))
             else:
-                c, h = x[1], x[2]
-                source = slope[K * c : K * (c + 1), N * h : N * (h + 1)]
-                nc.sync.dma_start(out=slopes[c, h][:], in_=source.rearrange("(p t) n -> p t n", t=PACK))
+                c, h, u = x[1:]
+                source = slope[K * c : K * (c + 1), :].rearrange("(p t) n -> p t n", t=PACK)[:, 2 * u : 2 * u + 2, :]
+                if h is not None:
+                    source = source[:, :, N * h : N * (h + 1)]
+                nc.sync.dma_start(out=slopes[c, h, u][:], in_=source)
 
-        nc.vector.memset(g_planes[:].rearrange("p g n -> p (g n)").bitcast(U32), 0)
         nc.vector.memset(cost_rows[:].bitcast(U32), 0)
+        for h in range(HALVES):
+            nc.vector.memset(g_planes[h][:].rearrange("p g n -> p (g n)").bitcast(U32), 0)
         make_identity(nc, identity[:])
 
-        load(("a", 0, 0))
         cost_partitions = slice(0, 4 * CHUNKS, 4)
-        nc.sync.dma_start(out=cost_rows[cost_partitions, :], in_=cost.rearrange("(c d) -> c d", c=CHUNKS))
-        load(("g", 0, slice(0, 1)))
-        for r in range(4):
-            nc.sync.dma_start(
-                out=g_planes[r:P:32, :, :].bitcast(I32),
-                in_=g_scales.bitcast(I32).rearrange("g (q r) n -> r q g n", r=4)[r],
-            )
         for x in [
-            ("a", 0, 1), ("g", 0, slice(1, 2)), ("slope", 0, 0),
-            ("a", 1, 0), ("g", 1, slice(0, 2)), ("slope", 0, 1),
-            ("a", 1, 1), ("a", 2, 0), ("slope", 1, 0),
-            ("a", 2, 1), ("slope", 1, 1),
-            ("w", 0), ("a", 3, 0), ("slope", 2, 0),
-            ("w", 1), ("a", 3, 1), ("slope", 2, 1),
-            ("w", 2), ("w", 3), ("slope", 3, 0), ("slope", 3, 1),
+            ("wide", 0), ("cost",), ("g", 0, slice(0, 1)), ("planes", 0), ("wide", 1), ("g", 0, slice(1, 2)), ("slope", 0, None, 0), ("slope", 0, None, 1), ("slope", 1, None, 0), ("slope", 1, None, 1), ("planes", 1), ("g", 1, slice(0, 2)), ("a", 2, 0), ("a", 2, 1), ("a", 3, 0), ("slope", 2, None, 0), ("slope", 2, None, 1), ("w", 0), ("a", 3, 1), ("w", 1), ("w", 2), ("slope", 3, None, 0), ("slope", 3, None, 1), ("w", 3),
         ]:
             load(x)
         nc.sync.dma_start(out=taus[:], in_=tau.rearrange("(p m) -> p m", m=PACK))
@@ -157,13 +172,13 @@ def tile_augmented_lagrangian_latent_gradient_e3_kernel(
             c, h = TILES[i]
             columns = slice(P * t, P * (t + 1))
             if g == 0:
-                banks[i, t] = psum.tile([P, N], F32, name="bank%d" % t)
+                banks[i, t] = psum.tile([P, N], F32, name=("sum%d" if i == 1 else "bank%d") % t)
             nc.tensor.matmul_mx(
                 out=banks[i, t][:],
                 lhsT=a_codes["a", c, g][:, columns].bitcast(E4M3),
                 lhsT_scale=a_planes["a", c, g][:, columns],
                 rhs=g_codes[h][:, g, :].bitcast(E5M2),
-                rhs_scale=g_planes[:, g, N * h : N * (h + 1)],
+                rhs_scale=g_planes[h][:, g, :],
                 start=(g == 0),
                 stop=(g == GROUPS - 1),
             )
@@ -172,20 +187,23 @@ def tile_augmented_lagrangian_latent_gradient_e3_kernel(
             pairs = [(t, g) for t in range(PACK) for g in range(GROUPS)]
             if TILES[i][1] == 0:
                 pairs = [(t, g) for g in range(GROUPS) for t in range(PACK)]
+            if i == 4:
+                pairs = [(2 * u + k, g) for u in range(2) for g in range(GROUPS) for k in range(2)]
             for t, g in pairs:
                 first_product(i, t, g)
 
         h_rows, h_grouped = {}, {}
 
-        def read_banks(i):
+        def read_banks(i, slots=range(PACK)):
             c, h = TILES[i]
-            h_rows[i] = stage.tile([P, PACK, N], BF16, name="h_rows", align_bytes=64, bufs=2)
-            for t in range(PACK):
+            if i not in h_rows:
+                h_rows[i] = stage.tile([P, PACK, N], BF16, name="h_rows", align_bytes=64, bufs=2)
+            for t in slots:
                 nc.vector.scalar_tensor_tensor(
                     out=h_rows[i][:, t, :],
                     in0=banks[i, t][:],
                     scalar=costs[:, t, c : c + 1],
-                    in1=slopes[c, h][:, t, :],
+                    in1=slope_row(c, h, t),
                     op0=ADD,
                     op1=MULT,
                 )
@@ -245,41 +263,57 @@ def tile_augmented_lagrangian_latent_gradient_e3_kernel(
         for t in range(PACK):
             nc.tensor.transpose(turned[:, t, :], cost_rows[:].rearrange("c (p t) -> c t p", t=PACK)[:, t, :], identity[:])
 
-        for g in range(GROUPS):
-            low, high = A_PIECES[0][2 * g : 2 * g + 2]
+        def quantise_slot(piece, k):
+            codes, planes, start = place(piece)
+            columns = slice(start + P * k, start + P * (k + 1))
+            nc.vector.quantize_mx(
+                out=codes[:, columns].bitcast(E4M3), scales=planes[:, columns], in_=grouped[piece][:, K * k : K * (k + 1)]
+            )
+
+        for c in range(2):
+            low, high = A_PIECES[c][:2]
             grouped[low], grouped[high] = piece_buffer(1)[:], piece_buffer(1)[:]
             interleave(low, both, "vector")
-            interleave(high, second, "scalar")
-            interleave(high, first, "vector")
-            if g == 0:
+            interleave(high, both, "scalar")
+            if c == 0:
                 nc.scalar.copy(costs[:], turned[:, :, cost_partitions])
-            quantise([low], grouped[low])
-            quantise([high], grouped[high])
-            for t in range(PACK):
-                first_product(0, t, g)
+        for c in range(2):
+            for piece in A_PIECES[c][:2]:
+                quantise([piece], grouped[piece])
+        for t in range(PACK):
+            first_product(0, t, 0)
+        low, high = A_PIECES[0][2:]
+        grouped[low], grouped[high] = piece_buffer(1)[:], piece_buffer(1)[:]
+        interleave(low, first, "vector")
+        interleave(high, second, "scalar")
+        interleave(low, second, "vector")
+        quantise_slot(low, 0)
+        interleave(high, first, "vector")
+        quantise_slot(low, 1)
+        quantise([high], grouped[high])
+        for t in range(PACK):
+            first_product(0, t, 1)
+        for t in range(PACK):
+            first_product(1, t, 0)
+        call = tuple(A_PIECES[1][2:])
+        buffer = piece_buffer(2)
+        for k, piece in enumerate(call):
+            grouped[piece] = buffer[:, 2 * K * k : 2 * K * (k + 1)]
+        interleave(call[0], both, "scalar")
+        interleave(call[1], first, "scalar")
+        interleave(call[1], second, "scalar")
+        read_banks(0, range(0, 2))
+        quantise(call, buffer[:])
+        for t in range(PACK):
+            first_product(1, t, 1)
+        read_banks(0, range(2, PACK))
+        first_products(2)
+        read_banks(1)
         for h in range(HALVES):
             for m in EARLY:
                 sums[h, m] = psum.tile([P, N], F32, name="sum%d" % (2 * h + m))
-
-        read_banks(0)
-        low, high = A_PIECES[1][:2]
-        grouped[low], grouped[high] = gate_buffer(0, 2 * K)[:], piece_buffer(1)[:]
-        interleave(low, both, "scalar")
-        interleave(high, both, "gpsimd")
-        quantise([low], grouped[low])
-        quantise([high], grouped[high])
-        first_products(1)
-        read_banks(1)
         share_h(0, N // 2)
-        low, high = A_PIECES[1][2:]
-        grouped[low], grouped[high] = piece_buffer(1)[:], gate_buffer(1, 2 * K)[:]
-        interleave(low, both, "scalar")
-        interleave(high, first, "gpsimd")
-        interleave(high, second, "vector")
-        quantise([low], grouped[low])
-        quantise([high], grouped[high])
         quantise_h(0, slice(0, N), h_grouped[0][:])
-        first_products(2)
 
         calls, buffers = {}, {}
         start = 0

@@ -26,19 +26,18 @@ HALVES = B // N
 
 TILES = [(0, 0), (1, 0), (0, 1), (1, 1), (2, 0), (2, 1), (3, 0), (3, 1)]
 LAST = len(TILES) - 1
-WHOLE_FROM = 0
+WHOLE_FROM = 2
 
 EARLY, LATE = range(0, 2), range(2, PACK)
 
 A_PIECES = [[(("a", c, g), u) for g in range(GROUPS) for u in range(2)] for c in range(CHUNKS)]
-BY_SLOTS = [(("a", 2, g), u) for u in range(2) for g in range(GROUPS)]
 W_EARLY = [(("w", c), 0) for c in range(CHUNKS)]
 W_LATE = [(("w", c), 1) for c in range(CHUNKS)]
-QUEUE = BY_SLOTS + A_PIECES[3][:2] + W_EARLY[:1] + A_PIECES[3][2:] + W_EARLY[1:2] + W_LATE[:2] + W_EARLY[2:] + W_LATE[2:]
-CALLS = {2: (1,), 3: (1, 1, 1), 4: (2, 1), 5: (2, 1), 6: (2, 1), 7: (1, 2)}
-AHEAD = 1
+QUEUE = A_PIECES[2] + A_PIECES[3][:2] + [W_EARLY[0], W_LATE[0]] + A_PIECES[3][2:] + W_EARLY[1:] + W_LATE[1:]
+CALLS = {2: (2,), 3: (1, 1), 4: (2, 1, 1), 5: (2, 1), 6: (2, 1), 7: (2,)}
+AHEAD = 2
 POOL_SHARE = 448
-LAST_SHARE = 160
+LAST_SHARE = 184
 
 
 def tile_augmented_lagrangian_latent_gradient_e3_kernel(
@@ -57,8 +56,8 @@ def tile_augmented_lagrangian_latent_gradient_e3_kernel(
         g_codes = [sbuf("g_codes%d" % h, [P, GROUPS, N], U32) for h in range(HALVES)]
         g_planes = [sbuf("g_planes%d" % h, [P, GROUPS, N], U8) for h in range(HALVES)]
         operands = [("a", c, g) for c in range(CHUNKS) for g in range(GROUPS)] + [("w", c) for c in range(CHUNKS)]
-        wide = [sbuf("wide%d" % g, [P, PACK, 2 * K], BF16) for g in range(GROUPS)]
-        raw = {("a", c, g): wide[g][:, :, K * c : K * (c + 1)] for c in range(2) for g in range(GROUPS)}
+        wide = [sbuf("wide0", [P, PACK, 2 * K], BF16)]
+        raw = {("a", c, 0): wide[0][:, :, K * c : K * (c + 1)] for c in range(2)}
         for n, x in enumerate(operands):
             if x not in raw:
                 raw[x] = sbuf("raw%d" % n, [P, PACK, K], BF16)
@@ -128,7 +127,7 @@ def tile_augmented_lagrangian_latent_gradient_e3_kernel(
 
         cost_partitions = slice(0, 4 * CHUNKS, 4)
         for x in [
-            ("wide", 0), ("cost",), ("g", 0, slice(0, 1)), ("planes", 0), ("wide", 1), ("g", 0, slice(1, 2)), ("slope", 0, None, 0), ("slope", 0, None, 1), ("slope", 1, None, 0), ("slope", 1, None, 1), ("planes", 1), ("g", 1, slice(0, 2)), ("a", 2, 0), ("a", 2, 1), ("a", 3, 0), ("slope", 2, None, 0), ("slope", 2, None, 1), ("w", 0), ("a", 3, 1), ("w", 1), ("w", 2), ("slope", 3, None, 0), ("slope", 3, None, 1), ("w", 3),
+            ("wide", 0), ("cost",), ("g", 0, slice(0, 1)), ("planes", 0), ("a", 0, 1), ("g", 0, slice(1, 2)), ("slope", 0, 0, 0), ("a", 1, 1), ("slope", 0, 0, 1), ("slope", 1, 0, 0), ("slope", 1, 0, 1), ("planes", 1), ("g", 1, slice(0, 2)), ("a", 2, 0), ("slope", 0, 1, 0), ("slope", 0, 1, 1), ("a", 2, 1), ("slope", 1, 1, 0), ("slope", 1, 1, 1), ("a", 3, 0), ("slope", 2, None, 0), ("w", 0), ("slope", 2, None, 1), ("a", 3, 1), ("w", 1), ("w", 2), ("w", 3), ("slope", 3, None, 0), ("slope", 3, None, 1),
         ]:
             load(x)
         nc.sync.dma_start(out=taus[:], in_=tau.rearrange("(p m) -> p m", m=PACK))
@@ -187,8 +186,6 @@ def tile_augmented_lagrangian_latent_gradient_e3_kernel(
             pairs = [(t, g) for t in range(PACK) for g in range(GROUPS)]
             if TILES[i][1] == 0:
                 pairs = [(t, g) for g in range(GROUPS) for t in range(PACK)]
-            if i == 4:
-                pairs = [(2 * u + k, g) for u in range(2) for g in range(GROUPS) for k in range(2)]
             for t, g in pairs:
                 first_product(i, t, g)
 
@@ -271,17 +268,22 @@ def tile_augmented_lagrangian_latent_gradient_e3_kernel(
             )
 
         for c in range(2):
-            low, high = A_PIECES[c][:2]
-            grouped[low], grouped[high] = piece_buffer(1)[:], piece_buffer(1)[:]
-            interleave(low, both, "vector")
-            interleave(high, both, "scalar")
-            if c == 0:
-                nc.scalar.copy(costs[:], turned[:, :, cost_partitions])
-        for c in range(2):
             for piece in A_PIECES[c][:2]:
-                quantise([piece], grouped[piece])
+                grouped[piece] = piece_buffer(1)[:]
+        low, high = A_PIECES[0][:2]
+        next_low, next_high = A_PIECES[1][:2]
+        interleave(low, both, "vector")
+        interleave(high, second, "scalar")
+        interleave(high, first, "vector")
+        interleave(next_low, both, "scalar")
+        nc.scalar.copy(costs[:], turned[:, :, cost_partitions])
+        interleave(next_high, first, "scalar")
+        quantise([low], grouped[low])
+        quantise([high], grouped[high])
         for t in range(PACK):
             first_product(0, t, 0)
+        interleave(next_high, second, "vector")
+        quantise([next_low], grouped[next_low])
         low, high = A_PIECES[0][2:]
         grouped[low], grouped[high] = piece_buffer(1)[:], piece_buffer(1)[:]
         interleave(low, first, "vector")
@@ -291,22 +293,22 @@ def tile_augmented_lagrangian_latent_gradient_e3_kernel(
         interleave(high, first, "vector")
         quantise_slot(low, 1)
         quantise([high], grouped[high])
+        quantise([next_high], grouped[next_high])
         for t in range(PACK):
             first_product(0, t, 1)
         for t in range(PACK):
             first_product(1, t, 0)
-        call = tuple(A_PIECES[1][2:])
-        buffer = piece_buffer(2)
-        for k, piece in enumerate(call):
-            grouped[piece] = buffer[:, 2 * K * k : 2 * K * (k + 1)]
-        interleave(call[0], both, "scalar")
-        interleave(call[1], first, "scalar")
-        interleave(call[1], second, "scalar")
-        read_banks(0, range(0, 2))
-        quantise(call, buffer[:])
+        low, high = A_PIECES[1][2:]
+        grouped[low], grouped[high] = piece_buffer(1)[:], gate_buffer(0, 2 * K)[:]
+        interleave(low, both, "scalar")
+        interleave(high, second, "gpsimd")
+        interleave(high, first, "scalar")
+        read_banks(0, range(0, 3))
+        quantise([low], grouped[low])
+        read_banks(0, range(3, PACK))
+        quantise([high], grouped[high])
         for t in range(PACK):
             first_product(1, t, 1)
-        read_banks(0, range(2, PACK))
         first_products(2)
         read_banks(1)
         for h in range(HALVES):
@@ -337,12 +339,12 @@ def tile_augmented_lagrangian_latent_gradient_e3_kernel(
         summed = []
         scalar_pieces(2, slice(0, AHEAD))
         for i in range(2, LAST + 1):
-            read_banks(i)
-            share_h(i - 1, POOL_SHARE)
+            read_banks(i, range(PACK if i < LAST else PACK - 1))
+            share_h(i - 1, POOL_SHARE if i < LAST else 272)
             scalar_pieces(i, slice(AHEAD, None))
             if i < LAST:
                 scalar_pieces(i + 1, slice(0, AHEAD))
-            for call in calls[i][: 1 if i == LAST else None]:
+            for call in calls[i] if i < LAST else []:
                 quantise(call, buffers[call][:])
                 for piece in call:
                     ready.add(piece)
@@ -356,6 +358,7 @@ def tile_augmented_lagrangian_latent_gradient_e3_kernel(
                         second_product(c, h, m)
                     summed.append((c, h))
 
+        read_banks(LAST, [PACK - 1])
         quantise(calls[LAST][-1], buffers[calls[LAST][-1]][:])
         middle = N // 2
         cut = middle + LAST_SHARE
@@ -363,13 +366,16 @@ def tile_augmented_lagrangian_latent_gradient_e3_kernel(
         interleave_h(LAST, slice(0, middle), parts[0][:], "scalar")
         interleave_h(LAST, slice(middle, cut), parts[1][:, : PACK * LAST_SHARE], "gpsimd")
         interleave_h(LAST, slice(cut, N), parts[1][:, PACK * LAST_SHARE :], "scalar")
-        for h in range(HALVES):
-            for m in LATE:
-                sums[h, m] = psum.tile([P, N], F32, name="bank%d" % (2 * h + m - 2))
-                for c in range(CHUNKS - 2):
-                    second_product(c, h, m)
+        def open_late(h, m):
+            sums[h, m] = psum.tile([P, N], F32, name="bank%d" % (2 * h + m - 2))
+            for c in range(CHUNKS - 2):
+                second_product(c, h, m)
+
+        for h, m in [(0, 2), (0, 3), (1, 2)]:
+            open_late(h, m)
         for m in EARLY:
             second_product(CHUNKS - 1, 0, m)
+        open_late(1, 3)
         for m in LATE:
             second_product(CHUNKS - 2, 0, m)
             second_product(CHUNKS - 1, 0, m)

@@ -153,8 +153,12 @@ def tile_augmented_lagrangian_latent_gradient_e3_kernel(
                     raw[x][:].rearrange("p j (m t) -> p t m j", t=PACK)[:, 2 * u : 2 * u + 2][:, slots],
                 )
                 return
-            dst = grouped[piece].rearrange("p (t m i j) -> p t m j i", t=2, i=2, j=PACK)[:, slots]
-            src = raw[x][:].rearrange("p j (m i t) -> p t m j i", i=2, t=PACK)[:, 2 * u : 2 * u + 2][:, slots]
+            if slots == both:
+                dst = grouped[piece].rearrange("p (t m i j) -> p m j i t", t=2, i=2, j=PACK)
+                src = raw[x][:].rearrange("p j (m i t) -> p m j i t", i=2, t=PACK)[:, :, :, :, 2 * u : 2 * u + 2]
+            else:
+                dst = grouped[piece].rearrange("p (t m i j) -> p t m j i", t=2, i=2, j=PACK)[:, slots]
+                src = raw[x][:].rearrange("p j (m i t) -> p t m j i", i=2, t=PACK)[:, 2 * u : 2 * u + 2][:, slots]
             if engine == "vector":
                 nc.vector.tensor_copy(out=dst, in_=src)
             else:

@@ -36,7 +36,7 @@ W_LATE = [(("w", c), 1) for c in range(CHUNKS)]
 QUEUE = A_PIECES[2] + A_PIECES[3][:2] + [W_EARLY[0], W_LATE[0]] + A_PIECES[3][2:] + W_EARLY[1:] + W_LATE[1:]
 CALLS = {2: (2,), 3: (1, 1), 4: (2, 1, 1), 5: (2, 1), 6: (2, 1), 7: (2,)}
 AHEAD = 2
-POOL_SHARE = 448
+POOL_SHARE = 432
 LAST_SHARE = 184
 
 
@@ -143,23 +143,19 @@ def tile_augmented_lagrangian_latent_gradient_e3_kernel(
             nc.gpsimd.tensor_scalar(out=dst, in0=src, scalar1=1.0, scalar2=0.0, op0=MULT, op1=ADD)
 
         grouped = {}
-        both, first, second = slice(0, 2), slice(0, 1), slice(1, 2)
+        first, second = slice(0, P // 4), slice(P // 4, P // 2)
 
-        def interleave(piece, slots, engine):
+        def interleave(piece, engine, pairs=slice(0, P // 2)):
             x, u = piece
+            dst = grouped[piece].rearrange("p (t m i j) -> p m j i t", t=2, i=2, j=PACK)[:, pairs]
+            src = raw[x][:].rearrange("p j (m i t) -> p m j i t", i=2, t=PACK)[:, pairs, :, :, 2 * u : 2 * u + 2]
             if engine == "gpsimd":
+                ms = slice(2 * pairs.start, 2 * pairs.stop)
                 pool_copy(
-                    grouped[piece].rearrange("p (t m j) -> p t m j", t=2, j=PACK)[:, slots],
-                    raw[x][:].rearrange("p j (m t) -> p t m j", t=PACK)[:, 2 * u : 2 * u + 2][:, slots],
+                    grouped[piece].rearrange("p (t m j) -> p m j t", t=2, j=PACK)[:, ms],
+                    raw[x][:].rearrange("p j (m t) -> p m j t", t=PACK)[:, ms, :, 2 * u : 2 * u + 2],
                 )
-                return
-            if slots == both:
-                dst = grouped[piece].rearrange("p (t m i j) -> p m j i t", t=2, i=2, j=PACK)
-                src = raw[x][:].rearrange("p j (m i t) -> p m j i t", i=2, t=PACK)[:, :, :, :, 2 * u : 2 * u + 2]
-            else:
-                dst = grouped[piece].rearrange("p (t m i j) -> p t m j i", t=2, i=2, j=PACK)[:, slots]
-                src = raw[x][:].rearrange("p j (m i t) -> p t m j i", i=2, t=PACK)[:, 2 * u : 2 * u + 2][:, slots]
-            if engine == "vector":
+            elif engine == "vector":
                 nc.vector.tensor_copy(out=dst, in_=src)
             else:
                 nc.scalar.copy(dst, src)
@@ -264,49 +260,40 @@ def tile_augmented_lagrangian_latent_gradient_e3_kernel(
         for t in range(PACK):
             nc.tensor.transpose(turned[:, t, :], cost_rows[:].rearrange("c (p t) -> c t p", t=PACK)[:, t, :], identity[:])
 
-        def quantise_slot(piece, k):
-            codes, planes, start = place(piece)
-            columns = slice(start + P * k, start + P * (k + 1))
-            nc.vector.quantize_mx(
-                out=codes[:, columns].bitcast(E4M3), scales=planes[:, columns], in_=grouped[piece][:, K * k : K * (k + 1)]
-            )
-
         for c in range(2):
             for piece in A_PIECES[c][:2]:
                 grouped[piece] = piece_buffer(1)[:]
         low, high = A_PIECES[0][:2]
         next_low, next_high = A_PIECES[1][:2]
-        interleave(low, both, "vector")
-        interleave(high, second, "scalar")
-        interleave(high, first, "vector")
-        interleave(next_low, both, "scalar")
+        interleave(low, "vector")
+        interleave(high, "scalar", second)
+        interleave(high, "vector", first)
+        interleave(next_low, "scalar")
         nc.scalar.copy(costs[:], turned[:, :, cost_partitions])
-        interleave(next_high, first, "scalar")
+        interleave(next_high, "scalar", first)
         quantise([low], grouped[low])
         quantise([high], grouped[high])
         for t in range(PACK):
             first_product(0, t, 0)
-        interleave(next_high, second, "vector")
+        interleave(next_high, "vector", second)
         quantise([next_low], grouped[next_low])
         low, high = A_PIECES[0][2:]
         grouped[low], grouped[high] = piece_buffer(1)[:], piece_buffer(1)[:]
-        interleave(low, first, "vector")
-        interleave(high, second, "scalar")
-        interleave(low, second, "vector")
-        quantise_slot(low, 0)
-        interleave(high, first, "vector")
-        quantise_slot(low, 1)
-        quantise([high], grouped[high])
+        interleave(low, "vector")
+        interleave(high, "scalar", slice(0, 48))
+        interleave(high, "vector", slice(48, P // 2))
+        quantise([low], grouped[low])
         quantise([next_high], grouped[next_high])
+        quantise([high], grouped[high])
         for t in range(PACK):
             first_product(0, t, 1)
         for t in range(PACK):
             first_product(1, t, 0)
         low, high = A_PIECES[1][2:]
         grouped[low], grouped[high] = piece_buffer(1)[:], gate_buffer(0, 2 * K)[:]
-        interleave(low, both, "scalar")
-        interleave(high, second, "gpsimd")
-        interleave(high, first, "scalar")
+        interleave(low, "scalar")
+        interleave(high, "gpsimd", slice(0, 24))
+        interleave(high, "scalar", slice(24, P // 2))
         read_banks(0, range(0, 3))
         quantise([low], grouped[low])
         read_banks(0, range(3, PACK))
@@ -337,7 +324,10 @@ def tile_augmented_lagrangian_latent_gradient_e3_kernel(
                     buffers[call] = gate_buffer(i, 2 * K * len(call)) if gate else piece_buffer(len(call))
                 k = call.index(piece)
                 grouped[piece] = buffers[call][:, 2 * K * k : 2 * K * (k + 1)]
-                interleave(piece, both, "scalar")
+                interleave(piece, "scalar")
+
+        def ahead(i):
+            return AHEAD if i < LAST else 1
 
         ready = {TILES[0]}
         summed = []
@@ -345,9 +335,9 @@ def tile_augmented_lagrangian_latent_gradient_e3_kernel(
         for i in range(2, LAST + 1):
             read_banks(i, range(PACK if i < LAST else PACK - 1))
             share_h(i - 1, POOL_SHARE if i < LAST else 272)
-            scalar_pieces(i, slice(AHEAD, None))
+            scalar_pieces(i, slice(ahead(i), None))
             if i < LAST:
-                scalar_pieces(i + 1, slice(0, AHEAD))
+                scalar_pieces(i + 1, slice(0, ahead(i + 1)))
             for call in calls[i] if i < LAST else []:
                 quantise(call, buffers[call][:])
                 for piece in call:

@@ -34,7 +34,7 @@ A_PIECES = [[(("a", c, g), u) for g in range(GROUPS) for u in range(2)] for c in
 W_EARLY = [(("w", c), 0) for c in range(CHUNKS)]
 W_LATE = [(("w", c), 1) for c in range(CHUNKS)]
 QUEUE = A_PIECES[2] + A_PIECES[3][:2] + [W_EARLY[0], W_LATE[0]] + A_PIECES[3][2:] + W_EARLY[1:] + W_LATE[1:]
-CALLS = {2: (2,), 3: (1, 1), 4: (2, 1, 1), 5: (2, 1), 6: (2, 1), 7: (2,)}
+CALLS = {2: (2,), 3: (1, 1, 1), 4: (1, 1, 1), 5: (1, 1, 1), 6: (2, 1), 7: (2,)}
 AHEAD = 2
 POOL_SHARE = 432
 LAST_SHARE = 184
@@ -273,27 +273,28 @@ def tile_augmented_lagrangian_latent_gradient_e3_kernel(
         interleave(next_high, "scalar", first)
         quantise([low], grouped[low])
         quantise([high], grouped[high])
-        for t in range(PACK):
+        for t in range(PACK - 1):
             first_product(0, t, 0)
         interleave(next_high, "vector", second)
         quantise([next_low], grouped[next_low])
         low, high = A_PIECES[0][2:]
         grouped[low], grouped[high] = piece_buffer(1)[:], piece_buffer(1)[:]
-        interleave(low, "vector")
+        interleave(low, "vector", slice(0, 42))
+        interleave(low, "scalar", slice(42, P // 2))
         interleave(high, "scalar", slice(0, 48))
-        interleave(high, "vector", slice(48, P // 2))
-        quantise([low], grouped[low])
         quantise([next_high], grouped[next_high])
+        quantise([low], grouped[low])
+        interleave(high, "vector", slice(48, P // 2))
         quantise([high], grouped[high])
-        for t in range(PACK):
-            first_product(0, t, 1)
+        for t, g in [(0, 1), (1, 1), (3, 0), (2, 1), (3, 1)]:
+            first_product(0, t, g)
         for t in range(PACK):
             first_product(1, t, 0)
         low, high = A_PIECES[1][2:]
         grouped[low], grouped[high] = piece_buffer(1)[:], gate_buffer(0, 2 * K)[:]
-        interleave(low, "scalar")
-        interleave(high, "gpsimd", slice(0, 24))
-        interleave(high, "scalar", slice(24, P // 2))
+        interleave(low, "gpsimd", slice(0, 24))
+        interleave(low, "scalar", slice(24, P // 2))
+        interleave(high, "scalar")
         read_banks(0, range(0, 3))
         quantise([low], grouped[low])
         read_banks(0, range(3, PACK))
@@ -365,23 +366,26 @@ def tile_augmented_lagrangian_latent_gradient_e3_kernel(
             for c in range(CHUNKS - 2):
                 second_product(c, h, m)
 
-        for h, m in [(0, 2), (0, 3), (1, 2)]:
-            open_late(h, m)
+        for m in LATE:
+            open_late(0, m)
         for m in EARLY:
             second_product(CHUNKS - 1, 0, m)
-        open_late(1, 3)
+        open_late(1, 2)
         for m in LATE:
             second_product(CHUNKS - 2, 0, m)
             second_product(CHUNKS - 1, 0, m)
-        for m in LATE:
-            second_product(CHUNKS - 2, 1, m)
+        open_late(1, 3)
+        second_product(CHUNKS - 2, 1, 2)
         for m in EARLY:
             finish(0, m)
         quantise_h(LAST, slice(0, middle), parts[0][:])
         quantise_h(LAST, slice(middle, N), parts[1][:])
         for m in LATE:
             finish(0, m)
-        for m in range(PACK):
+        for m in EARLY:
+            second_product(CHUNKS - 1, 1, m)
+        second_product(CHUNKS - 2, 1, 3)
+        for m in LATE:
             second_product(CHUNKS - 1, 1, m)
         for m in range(PACK):
             finish(1, m)

@@ -34,9 +34,9 @@ A_PIECES = [[(("a", c, g), u) for g in range(GROUPS) for u in range(2)] for c in
 W_EARLY = [(("w", c), 0) for c in range(CHUNKS)]
 W_LATE = [(("w", c), 1) for c in range(CHUNKS)]
 QUEUE = A_PIECES[2] + A_PIECES[3][:2] + [W_EARLY[0], W_LATE[0]] + A_PIECES[3][2:] + W_EARLY[1:] + W_LATE[1:]
-CALLS = {2: (2,), 3: (1, 1, 1), 4: (1, 1, 1), 5: (1, 1, 1), 6: (2, 1), 7: (2,)}
+CALLS = {2: (2,), 3: (1, 1), 4: (2, 1, 1), 5: (1, 1, 1), 6: (2, 1), 7: (2,)}
 AHEAD = 2
-POOL_SHARE = 432
+POOL_SHARE = 448
 LAST_SHARE = 184
 
 
@@ -156,7 +156,7 @@ def tile_augmented_lagrangian_latent_gradient_e3_kernel(
                     raw[x][:].rearrange("p j (m t) -> p m j t", t=PACK)[:, ms, :, 2 * u : 2 * u + 2],
                 )
             elif engine == "vector":
-                nc.vector.tensor_copy(out=dst, in_=src)
+                nc.vector.tensor_copy(out=dst.rearrange("p m j i t -> p t m j i"), in_=src.rearrange("p m j i t -> p t m j i"))
             else:
                 nc.scalar.copy(dst, src)
 

@@ -26,15 +26,15 @@ HALVES = B // N
 
 TILES = [(0, 0), (1, 0), (0, 1), (1, 1), (2, 0), (2, 1), (3, 0), (3, 1)]
 LAST = len(TILES) - 1
-WHOLE_FROM = 2
+WHOLE_FROM = 3
 
 EARLY, LATE = range(0, 2), range(2, PACK)
 
 A_PIECES = [[(("a", c, g), u) for g in range(GROUPS) for u in range(2)] for c in range(CHUNKS)]
 W_EARLY = [(("w", c), 0) for c in range(CHUNKS)]
 W_LATE = [(("w", c), 1) for c in range(CHUNKS)]
-QUEUE = A_PIECES[2] + A_PIECES[3][:2] + [W_EARLY[0], W_LATE[0]] + A_PIECES[3][2:] + W_EARLY[1:] + W_LATE[1:]
-CALLS = {2: (2,), 3: (1, 1), 4: (2, 1, 1), 5: (1, 1, 1), 6: (2, 1), 7: (2,)}
+QUEUE = A_PIECES[2] + A_PIECES[3][:2] + [W_EARLY[0], W_LATE[0]] + A_PIECES[3][2:] + W_EARLY[1:3] + [W_LATE[1], W_EARLY[3]] + W_LATE[2:]
+CALLS = {2: (2,), 3: (1, 1), 4: (2, 1, 1), 5: (1, 1, 1), 6: (1, 1), 7: (1, 2)}
 AHEAD = 2
 POOL_SHARE = 448
 LAST_SHARE = 184
@@ -127,7 +127,7 @@ def tile_augmented_lagrangian_latent_gradient_e3_kernel(
 
         cost_partitions = slice(0, 4 * CHUNKS, 4)
         for x in [
-            ("wide", 0), ("cost",), ("g", 0, slice(0, 1)), ("planes", 0), ("a", 0, 1), ("g", 0, slice(1, 2)), ("slope", 0, 0, 0), ("a", 1, 1), ("slope", 0, 0, 1), ("slope", 1, 0, 0), ("slope", 1, 0, 1), ("planes", 1), ("g", 1, slice(0, 2)), ("a", 2, 0), ("slope", 0, 1, 0), ("slope", 0, 1, 1), ("a", 2, 1), ("slope", 1, 1, 0), ("slope", 1, 1, 1), ("a", 3, 0), ("slope", 2, None, 0), ("w", 0), ("slope", 2, None, 1), ("a", 3, 1), ("w", 1), ("w", 2), ("w", 3), ("slope", 3, None, 0), ("slope", 3, None, 1),
+            ("wide", 0), ("cost",), ("g", 0, slice(0, 1)), ("planes", 0), ("a", 0, 1), ("g", 0, slice(1, 2)), ("slope", 0, 0, 0), ("a", 1, 1), ("slope", 0, 0, 1), ("slope", 1, 0, 0), ("slope", 1, 0, 1), ("planes", 1), ("g", 1, slice(0, 2)), ("a", 2, 0), ("slope", 0, 1, 0), ("slope", 0, 1, 1), ("a", 2, 1), ("slope", 1, 1, 0), ("slope", 1, 1, 1), ("a", 3, 0), ("slope", 2, 0, 0), ("w", 0), ("slope", 2, 0, 1), ("a", 3, 1), ("slope", 2, 1, 0), ("slope", 2, 1, 1), ("w", 1), ("w", 2), ("slope", 3, None, 0), ("slope", 3, None, 1), ("w", 3),
         ]:
             load(x)
         nc.sync.dma_start(out=taus[:], in_=tau.rearrange("(p m) -> p m", m=PACK))
@@ -328,7 +328,7 @@ def tile_augmented_lagrangian_latent_gradient_e3_kernel(
                 interleave(piece, "scalar")
 
         def ahead(i):
-            return AHEAD if i < LAST else 1
+            return AHEAD
 
         ready = {TILES[0]}
         summed = []
@@ -339,7 +339,7 @@ def tile_augmented_lagrangian_latent_gradient_e3_kernel(
             scalar_pieces(i, slice(ahead(i), None))
             if i < LAST:
                 scalar_pieces(i + 1, slice(0, ahead(i + 1)))
-            for call in calls[i] if i < LAST else []:
+            for call in calls[i][: 1 if i == LAST else None]:
                 quantise(call, buffers[call][:])
                 for piece in call:
                     ready.add(piece)

@@ -24,20 +24,28 @@ GROUPS = C // K
 CHUNKS = D // K
 HALVES = B // N
 
-TILES = [(0, 0), (1, 0), (0, 1), (1, 1), (2, 0), (2, 1), (3, 0), (3, 1)]
+PAIRS = P // 2
+
+TILES = [(c, h) for h in range(HALVES) for c in range(2)] + [(c, h) for c in range(2, CHUNKS) for h in range(HALVES)]
 LAST = len(TILES) - 1
-WHOLE_FROM = 3
 
 EARLY, LATE = range(0, 2), range(2, PACK)
 
 A_PIECES = [[(("a", c, g), u) for g in range(GROUPS) for u in range(2)] for c in range(CHUNKS)]
 W_EARLY = [(("w", c), 0) for c in range(CHUNKS)]
 W_LATE = [(("w", c), 1) for c in range(CHUNKS)]
-QUEUE = A_PIECES[2] + A_PIECES[3][:2] + [W_EARLY[0], W_LATE[0]] + A_PIECES[3][2:] + W_EARLY[1:3] + [W_LATE[1], W_EARLY[3]] + W_LATE[2:]
+QUEUE = (
+    A_PIECES[2] + A_PIECES[3][:2] + [W_EARLY[0], W_LATE[0]] + A_PIECES[3][2:]
+    + W_EARLY[1:3] + [W_LATE[1], W_EARLY[3]] + W_LATE[2:]
+)
 CALLS = {2: (2,), 3: (1, 1), 4: (2, 1, 1), 5: (1, 1, 1), 6: (1, 1), 7: (1, 2)}
 AHEAD = 2
 POOL_SHARE = 448
+BEFORE_LAST_SHARE = 272
 LAST_SHARE = 184
+VECTOR_PAIRS = 2 * PAIRS // 3
+SCALAR_PAIRS = 3 * PAIRS // 4
+POOL_PAIRS = 3 * PAIRS // 8
 
 
 def tile_augmented_lagrangian_latent_gradient_e3_kernel(
@@ -56,8 +64,8 @@ def tile_augmented_lagrangian_latent_gradient_e3_kernel(
         g_codes = [sbuf("g_codes%d" % h, [P, GROUPS, N], U32) for h in range(HALVES)]
         g_planes = [sbuf("g_planes%d" % h, [P, GROUPS, N], U8) for h in range(HALVES)]
         operands = [("a", c, g) for c in range(CHUNKS) for g in range(GROUPS)] + [("w", c) for c in range(CHUNKS)]
-        wide = [sbuf("wide0", [P, PACK, 2 * K], BF16)]
-        raw = {("a", c, 0): wide[0][:, :, K * c : K * (c + 1)] for c in range(2)}
+        opening = sbuf("wide0", [P, PACK, 2 * K], BF16)
+        raw = {("a", c, 0): opening[:, :, K * c : K * (c + 1)] for c in range(2)}
         for n, x in enumerate(operands):
             if x not in raw:
                 raw[x] = sbuf("raw%d" % n, [P, PACK, K], BF16)
@@ -72,14 +80,15 @@ def tile_augmented_lagrangian_latent_gradient_e3_kernel(
             if x[0] == "a":
                 return a_codes[x], a_planes[x], 2 * P * u
             return w_codes, w_planes, 2 * P * (W_EARLY + W_LATE).index(piece)
+
         slopes = {}
         for c in range(CHUNKS):
             for u in range(2):
-                for h in range(HALVES) if c < WHOLE_FROM else [None]:
+                for h in range(HALVES) if c < CHUNKS - 1 else [None]:
                     slopes[c, h, u] = sbuf("slopes%d%s%d" % (c, h, u), [P, 2, B if h is None else N], BF16)
 
         def slope_row(c, h, t):
-            if c < WHOLE_FROM:
+            if c < CHUNKS - 1:
                 return slopes[c, h, t // 2][:, t % 2, :]
             return slopes[c, None, t // 2][:, t % 2, N * h : N * (h + 1)]
 
@@ -90,11 +99,11 @@ def tile_augmented_lagrangian_latent_gradient_e3_kernel(
         identity = sbuf("identity", [P, P], BF16)
         taus = sbuf("taus", [P, PACK], BF16)
         z_rows = sbuf("z_rows", [P, PACK, B], BF16)
+        cost_partitions = slice(0, 4 * CHUNKS, 4)
 
         def load(x):
-            if x[0] == "wide":
-                source = a[K * x[1] : K * (x[1] + 1), : 2 * K]
-                nc.sync.dma_start(out=wide[x[1]][:], in_=source.rearrange("(p j) d -> p j d", j=PACK))
+            if x[0] == "opening":
+                nc.sync.dma_start(out=opening[:], in_=a[:K, : 2 * K].rearrange("(p j) d -> p j d", j=PACK))
             elif x[0] == "a":
                 c, g = x[1], x[2]
                 source = a[K * g : K * (g + 1), K * c : K * (c + 1)]
@@ -125,9 +134,16 @@ def tile_augmented_lagrangian_latent_gradient_e3_kernel(
             nc.vector.memset(g_planes[h][:].rearrange("p g n -> p (g n)").bitcast(U32), 0)
         make_identity(nc, identity[:])
 
-        cost_partitions = slice(0, 4 * CHUNKS, 4)
         for x in [
-            ("wide", 0), ("cost",), ("g", 0, slice(0, 1)), ("planes", 0), ("a", 0, 1), ("g", 0, slice(1, 2)), ("slope", 0, 0, 0), ("a", 1, 1), ("slope", 0, 0, 1), ("slope", 1, 0, 0), ("slope", 1, 0, 1), ("planes", 1), ("g", 1, slice(0, 2)), ("a", 2, 0), ("slope", 0, 1, 0), ("slope", 0, 1, 1), ("a", 2, 1), ("slope", 1, 1, 0), ("slope", 1, 1, 1), ("a", 3, 0), ("slope", 2, 0, 0), ("w", 0), ("slope", 2, 0, 1), ("a", 3, 1), ("slope", 2, 1, 0), ("slope", 2, 1, 1), ("w", 1), ("w", 2), ("slope", 3, None, 0), ("slope", 3, None, 1), ("w", 3),
+            ("opening",), ("cost",), ("g", 0, slice(0, 1)), ("planes", 0), ("a", 0, 1), ("g", 0, slice(1, 2)),
+            ("slope", 0, 0, 0), ("a", 1, 1), ("slope", 0, 0, 1),
+            ("slope", 1, 0, 0), ("slope", 1, 0, 1), ("planes", 1), ("g", 1, slice(0, 2)),
+            ("a", 2, 0), ("slope", 0, 1, 0), ("slope", 0, 1, 1),
+            ("a", 2, 1), ("slope", 1, 1, 0), ("slope", 1, 1, 1),
+            ("a", 3, 0), ("slope", 2, 0, 0), ("w", 0), ("slope", 2, 0, 1),
+            ("a", 3, 1), ("slope", 2, 1, 0), ("slope", 2, 1, 1),
+            ("w", 1), ("w", 2), ("slope", 3, None, 0), ("slope", 3, None, 1),
+            ("w", 3),
         ]:
             load(x)
         nc.sync.dma_start(out=taus[:], in_=tau.rearrange("(p m) -> p m", m=PACK))
@@ -143,20 +159,22 @@ def tile_augmented_lagrangian_latent_gradient_e3_kernel(
             nc.gpsimd.tensor_scalar(out=dst, in0=src, scalar1=1.0, scalar2=0.0, op0=MULT, op1=ADD)
 
         grouped = {}
-        first, second = slice(0, P // 4), slice(P // 4, P // 2)
 
-        def interleave(piece, engine, pairs=slice(0, P // 2)):
+        def interleave(piece, engine, pairs=slice(0, PAIRS)):
             x, u = piece
-            dst = grouped[piece].rearrange("p (t m i j) -> p m j i t", t=2, i=2, j=PACK)[:, pairs]
-            src = raw[x][:].rearrange("p j (m i t) -> p m j i t", i=2, t=PACK)[:, pairs, :, :, 2 * u : 2 * u + 2]
+            slots = slice(2 * u, 2 * u + 2)
             if engine == "gpsimd":
-                ms = slice(2 * pairs.start, 2 * pairs.stop)
+                columns = slice(2 * pairs.start, 2 * pairs.stop)
                 pool_copy(
-                    grouped[piece].rearrange("p (t m j) -> p m j t", t=2, j=PACK)[:, ms],
-                    raw[x][:].rearrange("p j (m t) -> p m j t", t=PACK)[:, ms, :, 2 * u : 2 * u + 2],
+                    grouped[piece].rearrange("p (t m j) -> p m j t", t=2, j=PACK)[:, columns],
+                    raw[x][:].rearrange("p j (m t) -> p m j t", t=PACK)[:, columns, :, slots],
                 )
-            elif engine == "vector":
-                nc.vector.tensor_copy(out=dst.rearrange("p m j i t -> p t m j i"), in_=src.rearrange("p m j i t -> p t m j i"))
+                return
+            dst = grouped[piece].rearrange("p (t m i j) -> p m j i t", t=2, i=2, j=PACK)[:, pairs]
+            src = raw[x][:].rearrange("p j (m i t) -> p m j i t", i=2, t=PACK)[:, pairs, :, :, slots]
+            if engine == "vector":
+                by_slot = "p m j i t -> p t m j i"
+                nc.vector.tensor_copy(out=dst.rearrange(by_slot), in_=src.rearrange(by_slot))
             else:
                 nc.scalar.copy(dst, src)
 
@@ -206,15 +224,12 @@ def tile_augmented_lagrangian_latent_gradient_e3_kernel(
                 )
 
         def interleave_h(i, columns, dst, engine):
-            src = h_rows[i][:, :, columns]
+            src = h_rows[i][:, :, columns].rearrange("p t (n i) -> p n t i", i=4)
+            dst = dst.rearrange("p (n i t) -> p n t i", i=4, t=PACK)
             if engine == "gpsimd":
-                pool_copy(
-                    dst.rearrange("p (n i t) -> p n t i", i=4, t=PACK), src.rearrange("p t (n i) -> p n t i", i=4)
-                )
+                pool_copy(dst, src)
             else:
-                nc.scalar.copy(
-                    dst.rearrange("p (n i t) -> p n t i", i=4, t=PACK), src.rearrange("p t (n i) -> p n t i", i=4)
-                )
+                nc.scalar.copy(dst, src)
 
         def share_h(i, share):
             h_grouped[i] = gate_buffer(i, PACK * N)
@@ -265,39 +280,42 @@ def tile_augmented_lagrangian_latent_gradient_e3_kernel(
                 grouped[piece] = piece_buffer(1)[:]
         low, high = A_PIECES[0][:2]
         next_low, next_high = A_PIECES[1][:2]
+        first_pairs, second_pairs = slice(0, PAIRS // 2), slice(PAIRS // 2, PAIRS)
         interleave(low, "vector")
-        interleave(high, "scalar", second)
-        interleave(high, "vector", first)
+        interleave(high, "scalar", second_pairs)
+        interleave(high, "vector", first_pairs)
         interleave(next_low, "scalar")
         nc.scalar.copy(costs[:], turned[:, :, cost_partitions])
-        interleave(next_high, "scalar", first)
+        interleave(next_high, "scalar", first_pairs)
         quantise([low], grouped[low])
         quantise([high], grouped[high])
         for t in range(PACK - 1):
             first_product(0, t, 0)
-        interleave(next_high, "vector", second)
+        interleave(next_high, "vector", second_pairs)
         quantise([next_low], grouped[next_low])
+
         low, high = A_PIECES[0][2:]
         grouped[low], grouped[high] = piece_buffer(1)[:], piece_buffer(1)[:]
-        interleave(low, "vector", slice(0, 42))
-        interleave(low, "scalar", slice(42, P // 2))
-        interleave(high, "scalar", slice(0, 48))
+        interleave(low, "vector", slice(0, VECTOR_PAIRS))
+        interleave(low, "scalar", slice(VECTOR_PAIRS, PAIRS))
+        interleave(high, "scalar", slice(0, SCALAR_PAIRS))
         quantise([next_high], grouped[next_high])
         quantise([low], grouped[low])
-        interleave(high, "vector", slice(48, P // 2))
+        interleave(high, "vector", slice(SCALAR_PAIRS, PAIRS))
         quantise([high], grouped[high])
         for t, g in [(0, 1), (1, 1), (3, 0), (2, 1), (3, 1)]:
             first_product(0, t, g)
         for t in range(PACK):
             first_product(1, t, 0)
+
         low, high = A_PIECES[1][2:]
         grouped[low], grouped[high] = piece_buffer(1)[:], gate_buffer(0, 2 * K)[:]
-        interleave(low, "gpsimd", slice(0, 24))
-        interleave(low, "scalar", slice(24, P // 2))
+        interleave(low, "gpsimd", slice(0, POOL_PAIRS))
+        interleave(low, "scalar", slice(POOL_PAIRS, PAIRS))
         interleave(high, "scalar")
-        read_banks(0, range(0, 3))
+        read_banks(0, range(PACK - 1))
         quantise([low], grouped[low])
-        read_banks(0, range(3, PACK))
+        read_banks(0, [PACK - 1])
         quantise([high], grouped[high])
         for t in range(PACK):
             first_product(1, t, 1)
@@ -318,7 +336,9 @@ def tile_augmented_lagrangian_latent_gradient_e3_kernel(
                 start += count
 
         def scalar_pieces(i, which):
-            for piece in [piece for call in calls[i] for piece in call][which]:
+            pieces = [piece for call in calls[i] for piece in call]
+            pieces = sorted(pieces, key=lambda piece: piece[0] == ("w", CHUNKS - 1))
+            for piece in pieces[which]:
                 call = [call for call in calls[i] if piece in call][0]
                 if piece == call[0]:
                     gate = call == calls[i][-1] and i < LAST
@@ -327,18 +347,15 @@ def tile_augmented_lagrangian_latent_gradient_e3_kernel(
                 grouped[piece] = buffers[call][:, 2 * K * k : 2 * K * (k + 1)]
                 interleave(piece, "scalar")
 
-        def ahead(i):
-            return AHEAD
-
         ready = {TILES[0]}
         summed = []
         scalar_pieces(2, slice(0, AHEAD))
         for i in range(2, LAST + 1):
             read_banks(i, range(PACK if i < LAST else PACK - 1))
-            share_h(i - 1, POOL_SHARE if i < LAST else 272)
-            scalar_pieces(i, slice(ahead(i), None))
+            share_h(i - 1, POOL_SHARE if i < LAST else BEFORE_LAST_SHARE)
+            scalar_pieces(i, slice(AHEAD, None))
             if i < LAST:
-                scalar_pieces(i + 1, slice(0, ahead(i + 1)))
+                scalar_pieces(i + 1, slice(0, AHEAD))
             for call in calls[i][: 1 if i == LAST else None]:
                 quantise(call, buffers[call][:])
                 for piece in call:
@@ -361,8 +378,9 @@ def tile_augmented_lagrangian_latent_gradient_e3_kernel(
         interleave_h(LAST, slice(0, middle), parts[0][:], "scalar")
         interleave_h(LAST, slice(middle, cut), parts[1][:, : PACK * LAST_SHARE], "gpsimd")
         interleave_h(LAST, slice(cut, N), parts[1][:, PACK * LAST_SHARE :], "scalar")
+
         def open_late(h, m):
-            sums[h, m] = psum.tile([P, N], F32, name="bank%d" % (2 * h + m - 2))
+            sums[h, m] = psum.tile([P, N], F32, name="bank%d" % (len(LATE) * h + LATE.index(m)))
             for c in range(CHUNKS - 2):
                 second_product(c, h, m)
 
@@ -370,12 +388,12 @@ def tile_augmented_lagrangian_latent_gradient_e3_kernel(
             open_late(0, m)
         for m in EARLY:
             second_product(CHUNKS - 1, 0, m)
-        open_late(1, 2)
+        open_late(1, LATE[0])
         for m in LATE:
             second_product(CHUNKS - 2, 0, m)
             second_product(CHUNKS - 1, 0, m)
-        open_late(1, 3)
-        second_product(CHUNKS - 2, 1, 2)
+        open_late(1, LATE[1])
+        second_product(CHUNKS - 2, 1, LATE[0])
         for m in EARLY:
             finish(0, m)
         quantise_h(LAST, slice(0, middle), parts[0][:])
@@ -384,7 +402,7 @@ def tile_augmented_lagrangian_latent_gradient_e3_kernel(
             finish(0, m)
         for m in EARLY:
             second_product(CHUNKS - 1, 1, m)
-        second_product(CHUNKS - 2, 1, 3)
+        second_product(CHUNKS - 2, 1, LATE[1])
         for m in LATE:
             second_product(CHUNKS - 1, 1, m)
         for m in range(PACK):

@@ -35,10 +35,10 @@ A_PIECES = [[(("a", c, g), u) for g in range(GROUPS) for u in range(2)] for c in
 W_EARLY = [(("w", c), 0) for c in range(CHUNKS)]
 W_LATE = [(("w", c), 1) for c in range(CHUNKS)]
 QUEUE = (
-    A_PIECES[2] + A_PIECES[3][:2] + [W_EARLY[0], W_LATE[0]] + A_PIECES[3][2:]
-    + W_EARLY[1:3] + [W_LATE[1], W_EARLY[3]] + W_LATE[2:]
+    A_PIECES[2] + W_EARLY[:1] + A_PIECES[3][:2] + W_EARLY[1:2] + A_PIECES[3][2:]
+    + W_EARLY[2:3] + W_LATE[:2] + W_EARLY[3:] + W_LATE[2:]
 )
-CALLS = {2: (2,), 3: (1, 1), 4: (2, 1, 1), 5: (1, 1, 1), 6: (1, 1), 7: (1, 2)}
+CALLS = {2: (2,), 3: (1, 1, 1), 4: (2, 1), 5: (1, 1, 1), 6: (2,), 7: (1, 2)}
 AHEAD = 2
 POOL_SHARE = 448
 BEFORE_LAST_SHARE = 272
@@ -140,9 +140,9 @@ def tile_augmented_lagrangian_latent_gradient_e3_kernel(
             ("slope", 1, 0, 0), ("slope", 1, 0, 1), ("planes", 1), ("g", 1, slice(0, 2)),
             ("a", 2, 0), ("slope", 0, 1, 0), ("slope", 0, 1, 1),
             ("a", 2, 1), ("slope", 1, 1, 0), ("slope", 1, 1, 1),
-            ("a", 3, 0), ("slope", 2, 0, 0), ("w", 0), ("slope", 2, 0, 1),
-            ("a", 3, 1), ("slope", 2, 1, 0), ("slope", 2, 1, 1),
-            ("w", 1), ("w", 2), ("slope", 3, None, 0), ("slope", 3, None, 1),
+            ("w", 0), ("a", 3, 0), ("slope", 2, 0, 0), ("slope", 2, 0, 1),
+            ("w", 1), ("a", 3, 1), ("slope", 2, 1, 0), ("slope", 2, 1, 1),
+            ("w", 2), ("slope", 3, None, 0), ("slope", 3, None, 1),
             ("w", 3),
         ]:
             load(x)
@@ -386,13 +386,13 @@ def tile_augmented_lagrangian_latent_gradient_e3_kernel(
 
         for m in LATE:
             open_late(0, m)
+        open_late(1, LATE[0])
         for m in EARLY:
             second_product(CHUNKS - 1, 0, m)
-        open_late(1, LATE[0])
+        open_late(1, LATE[1])
         for m in LATE:
             second_product(CHUNKS - 2, 0, m)
             second_product(CHUNKS - 1, 0, m)
-        open_late(1, LATE[1])
         second_product(CHUNKS - 2, 1, LATE[0])
         for m in EARLY:
             finish(0, m)

@@ -170,10 +170,10 @@ def tile_augmented_lagrangian_latent_gradient_e3_kernel(
                     raw[x][:].rearrange("p j (m t) -> p m j t", t=PACK)[:, columns, :, slots],
                 )
                 return
-            dst = grouped[piece].rearrange("p (t m i j) -> p m j i t", t=2, i=2, j=PACK)[:, pairs]
-            src = raw[x][:].rearrange("p j (m i t) -> p m j i t", i=2, t=PACK)[:, pairs, :, :, slots]
+            dst = grouped[piece].rearrange("p (t m i j) -> p m j t i", t=2, i=2, j=PACK)[:, pairs]
+            src = raw[x][:].rearrange("p j (m i t) -> p m j t i", i=2, t=PACK)[:, pairs, :, slots, :]
             if engine == "vector":
-                by_slot = "p m j i t -> p t m j i"
+                by_slot = "p m j t i -> p t m j i"
                 nc.vector.tensor_copy(out=dst.rearrange(by_slot), in_=src.rearrange(by_slot))
             else:
                 nc.scalar.copy(dst, src)

@@ -40,11 +40,9 @@ QUEUE = (
 )
 CALLS = {2: (2,), 3: (1, 1, 1), 4: (2, 1), 5: (1, 1, 1), 6: (2,), 7: (1, 2)}
 AHEAD = 2
-POOL_SHARE = 448
+POOL_SHARE = 440
 BEFORE_LAST_SHARE = 272
 LAST_SHARE = 184
-VECTOR_PAIRS = 2 * PAIRS // 3
-SCALAR_PAIRS = 3 * PAIRS // 4
 POOL_PAIRS = 3 * PAIRS // 8
 
 
@@ -178,6 +176,22 @@ def tile_augmented_lagrangian_latent_gradient_e3_kernel(
             else:
                 nc.scalar.copy(dst, src)
 
+        def interleave_slot(piece, t, engine):
+            x, u = piece
+            dst = grouped[piece].rearrange("p (t m i j) -> p t m j i", t=2, i=2, j=PACK)[:, t]
+            src = raw[x][:].rearrange("p j (m i t) -> p t m j i", i=2, t=PACK)[:, 2 * u + t]
+            if engine == "vector":
+                nc.vector.tensor_copy(out=dst, in_=src)
+            else:
+                nc.scalar.copy(dst, src)
+
+        def quantise_slot(piece, t):
+            codes, planes, start = place(piece)
+            columns = slice(start + P * t, start + P * (t + 1))
+            nc.vector.quantize_mx(
+                out=codes[:, columns].bitcast(E4M3), scales=planes[:, columns], in_=grouped[piece][:, K * t : K * (t + 1)]
+            )
+
         def quantise(call, source):
             codes, planes, start = place(call[0])
             columns = slice(start, start + 2 * P * len(call))
@@ -296,12 +310,13 @@ def tile_augmented_lagrangian_latent_gradient_e3_kernel(
 
         low, high = A_PIECES[0][2:]
         grouped[low], grouped[high] = piece_buffer(1)[:], piece_buffer(1)[:]
-        interleave(low, "vector", slice(0, VECTOR_PAIRS))
-        interleave(low, "scalar", slice(VECTOR_PAIRS, PAIRS))
-        interleave(high, "scalar", slice(0, SCALAR_PAIRS))
+        interleave_slot(low, 0, "vector")
+        interleave_slot(low, 1, "scalar")
+        interleave(high, "scalar", first_pairs)
         quantise([next_high], grouped[next_high])
-        quantise([low], grouped[low])
-        interleave(high, "vector", slice(SCALAR_PAIRS, PAIRS))
+        quantise_slot(low, 0)
+        interleave(high, "vector", second_pairs)
+        quantise_slot(low, 1)
         quantise([high], grouped[high])
         for t, g in [(0, 1), (1, 1), (3, 0), (2, 1), (3, 1)]:
             first_product(0, t, g)
@@ -372,12 +387,13 @@ def tile_augmented_lagrangian_latent_gradient_e3_kernel(
 
         read_banks(LAST, [PACK - 1])
         quantise(calls[LAST][-1], buffers[calls[LAST][-1]][:])
-        middle = N // 2
-        cut = middle + LAST_SHARE
-        parts = [piece_buffer(1), gate_buffer(LAST - 1, 2 * K)]
-        interleave_h(LAST, slice(0, middle), parts[0][:], "scalar")
-        interleave_h(LAST, slice(middle, cut), parts[1][:, : PACK * LAST_SHARE], "gpsimd")
-        interleave_h(LAST, slice(cut, N), parts[1][:, PACK * LAST_SHARE :], "scalar")
+        quarter = N // 4
+        cut = quarter + LAST_SHARE
+        parts = [piece_buffer(1), gate_buffer(LAST - 1, 2 * K), piece_buffer(1)]
+        interleave_h(LAST, slice(0, quarter), parts[0][:, :K], "scalar")
+        interleave_h(LAST, slice(quarter, cut), parts[1][:, : PACK * LAST_SHARE], "gpsimd")
+        interleave_h(LAST, slice(cut, 3 * quarter), parts[1][:, PACK * LAST_SHARE :], "scalar")
+        interleave_h(LAST, slice(3 * quarter, N), parts[2][:, :K], "scalar")
 
         def open_late(h, m):
             sums[h, m] = psum.tile([P, N], F32, name="bank%d" % (len(LATE) * h + LATE.index(m)))
@@ -396,8 +412,9 @@ def tile_augmented_lagrangian_latent_gradient_e3_kernel(
         second_product(CHUNKS - 2, 1, LATE[0])
         for m in EARLY:
             finish(0, m)
-        quantise_h(LAST, slice(0, middle), parts[0][:])
-        quantise_h(LAST, slice(middle, N), parts[1][:])
+        quantise_h(LAST, slice(0, quarter), parts[0][:, :K])
+        quantise_h(LAST, slice(quarter, 3 * quarter), parts[1][:])
+        quantise_h(LAST, slice(3 * quarter, N), parts[2][:, :K])
         for m in LATE:
             finish(0, m)
         for m in EARLY:

from contextlib import ExitStack

import concourse.mybir as mybir
from concourse.masks import make_identity

C, D, L, B = 1024, 2048, 512, 1024
FLOPS = 2 * C * D * B + 2 * D * L * B

F32 = mybir.dt.float32
BF16 = mybir.dt.bfloat16
I32 = mybir.dt.int32
U32 = mybir.dt.uint32
U8 = mybir.dt.uint8
E4M3 = mybir.dt.float8_e4m3fn_x4
E5M2 = mybir.dt.float8_e5m2_x4
ADD = mybir.AluOpType.add
MULT = mybir.AluOpType.mult

P = 128
PACK = 4
K = P * PACK
N = 512
GROUPS = C // K
CHUNKS = D // K
HALVES = B // N

PAIRS = P // 2

TILES = [(c, h) for h in range(HALVES) for c in range(2)] + [(c, h) for c in range(2, CHUNKS) for h in range(HALVES)]
LAST = len(TILES) - 1

EARLY, LATE = range(0, 2), range(2, PACK)

A_PIECES = [[(("a", c, g), u) for g in range(GROUPS) for u in range(2)] for c in range(CHUNKS)]
W_EARLY = [(("w", c), 0) for c in range(CHUNKS)]
W_LATE = [(("w", c), 1) for c in range(CHUNKS)]
QUEUE = (
    A_PIECES[2] + W_EARLY[:1] + A_PIECES[3][:2] + W_EARLY[1:2] + A_PIECES[3][2:]
    + W_EARLY[2:3] + W_LATE[:2] + W_EARLY[3:] + W_LATE[2:]
)
CALLS = {2: (2,), 3: (1, 1, 1), 4: (2, 1), 5: (1, 1, 1), 6: (2,), 7: (1, 2)}
AHEAD = 2
POOL_SHARE = 440
BEFORE_LAST_SHARE = 272
LAST_SHARE = 184
POOL_PAIRS = 3 * PAIRS // 8


def tile_augmented_lagrangian_latent_gradient_e3_kernel(
    tc, g_words, g_scales, a, cost, slope, w, tau, z, out
):
    nc = tc.nc
    with ExitStack() as ctx:
        keep = ctx.enter_context(tc.tile_pool(name="keep", bufs=1))
        stage = ctx.enter_context(tc.tile_pool(name="stage", bufs=1))
        psum = ctx.enter_context(tc.psum_pool(name="psum", bufs=1))
        ctx.enter_context(tc.manual_schedule())

        def sbuf(name, shape, dtype):
            return keep.tile(shape, dtype, name=name, align_bytes=64)

        g_codes = [sbuf("g_codes%d" % h, [P, GROUPS, N], U32) for h in range(HALVES)]
        g_planes = [sbuf("g_planes%d" % h, [P, GROUPS, N], U8) for h in range(HALVES)]
        operands = [("a", c, g) for c in range(CHUNKS) for g in range(GROUPS)] + [("w", c) for c in range(CHUNKS)]
        opening = sbuf("wide0", [P, PACK, 2 * K], BF16)
        raw = {("a", c, 0): opening[:, :, K * c : K * (c + 1)] for c in range(2)}
        for n, x in enumerate(operands):
            if x not in raw:
                raw[x] = sbuf("raw%d" % n, [P, PACK, K], BF16)
        a_operands = operands[: CHUNKS * GROUPS]
        a_codes = {x: sbuf("codes%d" % n, [P, K], U32) for n, x in enumerate(a_operands)}
        a_planes = {x: sbuf("planes%d" % n, [P, K], U8) for n, x in enumerate(a_operands)}
        w_codes = sbuf("w_codes", [P, CHUNKS * L], U32)
        w_planes = sbuf("w_planes", [P, CHUNKS * L], U8)

        def place(piece):
            x, u = piece
            if x[0] == "a":
                return a_codes[x], a_planes[x], 2 * P * u
            return w_codes, w_planes, 2 * P * (W_EARLY + W_LATE).index(piece)

        slopes = {}
        for c in range(CHUNKS):
            for u in range(2):
                for h in range(HALVES) if c < CHUNKS - 1 else [None]:
                    slopes[c, h, u] = sbuf("slopes%d%s%d" % (c, h, u), [P, 2, B if h is None else N], BF16)

        def slope_row(c, h, t):
            if c < CHUNKS - 1:
                return slopes[c, h, t // 2][:, t % 2, :]
            return slopes[c, None, t // 2][:, t % 2, N * h : N * (h + 1)]

        h_codes = {tile: sbuf("h_codes%d%d" % tile, [P, N], U32) for tile in TILES}
        h_planes = {tile: sbuf("h_planes%d%d" % tile, [P, N], U8) for tile in TILES}
        cost_rows = sbuf("cost_rows", [P, K], BF16)
        costs = sbuf("costs", [P, PACK, CHUNKS], BF16)
        identity = sbuf("identity", [P, P], BF16)
        taus = sbuf("taus", [P, PACK], BF16)
        z_rows = sbuf("z_rows", [P, PACK, B], BF16)
        cost_partitions = slice(0, 4 * CHUNKS, 4)

        def load(x):
            if x[0] == "opening":
                nc.sync.dma_start(out=opening[:], in_=a[:K, : 2 * K].rearrange("(p j) d -> p j d", j=PACK))
            elif x[0] == "a":
                c, g = x[1], x[2]
                source = a[K * g : K * (g + 1), K * c : K * (c + 1)]
                nc.sync.dma_start(out=raw[x][:], in_=source.rearrange("(p j) d -> p j d", j=PACK))
            elif x[0] == "w":
                source = w[K * x[1] : K * (x[1] + 1), :]
                nc.sync.dma_start(out=raw[x][:], in_=source.rearrange("(p j) l -> p j l", j=PACK))
            elif x[0] == "g":
                h, groups = x[1], x[2]
                source = g_words.rearrange("g p n t -> p g (n t)")[:, groups, PACK * N * h : PACK * N * (h + 1)]
                nc.sync.dma_start(out=g_codes[h][:, groups, :].bitcast(I32), in_=source.bitcast(I32))
            elif x[0] == "planes":
                h = x[1]
                rows = g_scales[:, :, N * h : N * (h + 1)].bitcast(I32).rearrange("g (q r) n -> r q g n", r=4)
                for r in range(4):
                    nc.sync.dma_start(out=g_planes[h][r:P:32, :, :].bitcast(I32), in_=rows[r])
            elif x[0] == "cost":
                nc.sync.dma_start(out=cost_rows[cost_partitions, :], in_=cost.rearrange("(c d) -> c d", c=CHUNKS))
            else:
                c, h, u = x[1:]
                source = slope[K * c : K * (c + 1), :].rearrange("(p t) n -> p t n", t=PACK)[:, 2 * u : 2 * u + 2, :]
                if h is not None:
                    source = source[:, :, N * h : N * (h + 1)]
                nc.sync.dma_start(out=slopes[c, h, u][:], in_=source)

        nc.vector.memset(cost_rows[:].bitcast(U32), 0)
        for h in range(HALVES):
            nc.vector.memset(g_planes[h][:].rearrange("p g n -> p (g n)").bitcast(U32), 0)
        make_identity(nc, identity[:])

        for x in [
            ("opening",), ("cost",), ("g", 0, slice(0, 1)), ("planes", 0), ("a", 0, 1), ("g", 0, slice(1, 2)),
            ("slope", 0, 0, 0), ("a", 1, 1), ("slope", 0, 0, 1),
            ("slope", 1, 0, 0), ("slope", 1, 0, 1), ("planes", 1), ("g", 1, slice(0, 2)),
            ("a", 2, 0), ("slope", 0, 1, 0), ("slope", 0, 1, 1),
            ("a", 2, 1), ("slope", 1, 1, 0), ("slope", 1, 1, 1),
            ("w", 0), ("a", 3, 0), ("slope", 2, 0, 0), ("slope", 2, 0, 1),
            ("w", 1), ("a", 3, 1), ("slope", 2, 1, 0), ("slope", 2, 1, 1),
            ("w", 2), ("slope", 3, None, 0), ("slope", 3, None, 1),
            ("w", 3),
        ]:
            load(x)
        nc.sync.dma_start(out=taus[:], in_=tau.rearrange("(p m) -> p m", m=PACK))
        nc.sync.dma_start(out=z_rows[:], in_=z.rearrange("(p m) n -> p m n", m=PACK))

        def piece_buffer(count):
            return stage.tile([P, 2 * K * count], BF16, name="piece", align_bytes=64, bufs=4)

        def gate_buffer(i, width):
            return stage.tile([P, width], BF16, name="gate%d" % (i % 3), align_bytes=64, bufs=1)

        def pool_copy(dst, src):
            nc.gpsimd.tensor_scalar(out=dst, in0=src, scalar1=1.0, scalar2=0.0, op0=MULT, op1=ADD)

        grouped = {}

        def interleave(piece, engine, pairs=slice(0, PAIRS)):
            x, u = piece
            slots = slice(2 * u, 2 * u + 2)
            if engine == "gpsimd":
                columns = slice(2 * pairs.start, 2 * pairs.stop)
                pool_copy(
                    grouped[piece].rearrange("p (t m j) -> p m j t", t=2, j=PACK)[:, columns],
                    raw[x][:].rearrange("p j (m t) -> p m j t", t=PACK)[:, columns, :, slots],
                )
                return
            dst = grouped[piece].rearrange("p (t m i j) -> p m j t i", t=2, i=2, j=PACK)[:, pairs]
            src = raw[x][:].rearrange("p j (m i t) -> p m j t i", i=2, t=PACK)[:, pairs, :, slots, :]
            if engine == "vector":
                by_slot = "p m j t i -> p t m j i"
                nc.vector.tensor_copy(out=dst.rearrange(by_slot), in_=src.rearrange(by_slot))
            else:
                nc.scalar.copy(dst, src)

        def interleave_slot(piece, t, engine):
            x, u = piece
            dst = grouped[piece].rearrange("p (t m i j) -> p t m j i", t=2, i=2, j=PACK)[:, t]
            src = raw[x][:].rearrange("p j (m i t) -> p t m j i", i=2, t=PACK)[:, 2 * u + t]
            if engine == "vector":
                nc.vector.tensor_copy(out=dst, in_=src)
            else:
                nc.scalar.copy(dst, src)

        def quantise_slot(piece, t):
            codes, planes, start = place(piece)
            columns = slice(start + P * t, start + P * (t + 1))
            nc.vector.quantize_mx(
                out=codes[:, columns].bitcast(E4M3), scales=planes[:, columns], in_=grouped[piece][:, K * t : K * (t + 1)]
            )

        def quantise(call, source):
            codes, planes, start = place(call[0])
            columns = slice(start, start + 2 * P * len(call))
            nc.vector.quantize_mx(out=codes[:, columns].bitcast(E4M3), scales=planes[:, columns], in_=source)

        banks = {}

        def first_product(i, t, g):
            c, h = TILES[i]
            columns = slice(P * t, P * (t + 1))
            if g == 0:
                banks[i, t] = psum.tile([P, N], F32, name=("sum%d" if i == 1 else "bank%d") % t)
            nc.tensor.matmul_mx(
                out=banks[i, t][:],
                lhsT=a_codes["a", c, g][:, columns].bitcast(E4M3),
                lhsT_scale=a_planes["a", c, g][:, columns],
                rhs=g_codes[h][:, g, :].bitcast(E5M2),
                rhs_scale=g_planes[h][:, g, :],
                start=(g == 0),
                stop=(g == GROUPS - 1),
            )

        def first_products(i):
            pairs = [(t, g) for t in range(PACK) for g in range(GROUPS)]
            if TILES[i][1] == 0:
                pairs = [(t, g) for g in range(GROUPS) for t in range(PACK)]
            for t, g in pairs:
                first_product(i, t, g)

        h_rows, h_grouped = {}, {}

        def read_banks(i, slots=range(PACK)):
            c, h = TILES[i]
            if i not in h_rows:
                h_rows[i] = stage.tile([P, PACK, N], BF16, name="h_rows", align_bytes=64, bufs=2)
            for t in slots:
                nc.vector.scalar_tensor_tensor(
                    out=h_rows[i][:, t, :],
                    in0=banks[i, t][:],
                    scalar=costs[:, t, c : c + 1],
                    in1=slope_row(c, h, t),
                    op0=ADD,
                    op1=MULT,
                )

        def interleave_h(i, columns, dst, engine):
            src = h_rows[i][:, :, columns].rearrange("p t (n i) -> p n t i", i=4)
            dst = dst.rearrange("p (n i t) -> p n t i", i=4, t=PACK)
            if engine == "gpsimd":
                pool_copy(dst, src)
            else:
                nc.scalar.copy(dst, src)

        def share_h(i, share):
            h_grouped[i] = gate_buffer(i, PACK * N)
            interleave_h(i, slice(0, share), h_grouped[i][:, : PACK * share], "gpsimd")
            interleave_h(i, slice(share, N), h_grouped[i][:, PACK * share :], "scalar")

        def quantise_h(i, columns, source):
            nc.vector.quantize_mx(
                out=h_codes[TILES[i]][:, columns].bitcast(E5M2), scales=h_planes[TILES[i]][:, columns], in_=source
            )

        sums = {}

        def second_product(c, h, m):
            start = place((("w", c), m // 2))[2] + P * (m % 2)
            columns = slice(start, start + P)
            nc.tensor.matmul_mx(
                out=sums[h, m][:],
                lhsT=w_codes[:, columns].bitcast(E4M3),
                lhsT_scale=w_planes[:, columns],
                rhs=h_codes[c, h][:].bitcast(E5M2),
                rhs_scale=h_planes[c, h][:],
                start=(c == 0),
                stop=(c == CHUNKS - 1),
            )

        out_rows = out.rearrange("(p m) n -> p m n", m=PACK)

        def finish(h, m):
            columns = slice(N * h, N * (h + 1))
            result = stage.tile([P, N], F32, name="result", align_bytes=64, bufs=HALVES * PACK)
            nc.vector.scalar_tensor_tensor(
                out=result[:],
                in0=z_rows[:, m, columns],
                scalar=taus[:, m : m + 1],
                in1=sums[h, m][:],
                op0=MULT,
                op1=ADD,
            )
            nc.sync.dma_start(out=out_rows[:, m, columns], in_=result[:])

        turned = psum.tile([P, PACK, P], BF16, name="sum0")
        for t in range(PACK):
            nc.tensor.transpose(turned[:, t, :], cost_rows[:].rearrange("c (p t) -> c t p", t=PACK)[:, t, :], identity[:])

        for c in range(2):
            for piece in A_PIECES[c][:2]:
                grouped[piece] = piece_buffer(1)[:]
        low, high = A_PIECES[0][:2]
        next_low, next_high = A_PIECES[1][:2]
        first_pairs, second_pairs = slice(0, PAIRS // 2), slice(PAIRS // 2, PAIRS)
        interleave(low, "vector")
        interleave(high, "scalar", second_pairs)
        interleave(high, "vector", first_pairs)
        interleave(next_low, "scalar")
        nc.scalar.copy(costs[:], turned[:, :, cost_partitions])
        interleave(next_high, "scalar", first_pairs)
        quantise([low], grouped[low])
        quantise([high], grouped[high])
        for t in range(PACK - 1):
            first_product(0, t, 0)
        interleave(next_high, "vector", second_pairs)
        quantise([next_low], grouped[next_low])

        low, high = A_PIECES[0][2:]
        grouped[low], grouped[high] = piece_buffer(1)[:], piece_buffer(1)[:]
        interleave_slot(low, 0, "vector")
        interleave_slot(low, 1, "scalar")
        interleave(high, "scalar", first_pairs)
        quantise([next_high], grouped[next_high])
        quantise_slot(low, 0)
        interleave(high, "vector", second_pairs)
        quantise_slot(low, 1)
        quantise([high], grouped[high])
        for t, g in [(0, 1), (1, 1), (3, 0), (2, 1), (3, 1)]:
            first_product(0, t, g)
        for t in range(PACK):
            first_product(1, t, 0)

        low, high = A_PIECES[1][2:]
        grouped[low], grouped[high] = piece_buffer(1)[:], gate_buffer(0, 2 * K)[:]
        interleave(low, "gpsimd", slice(0, POOL_PAIRS))
        interleave(low, "scalar", slice(POOL_PAIRS, PAIRS))
        interleave(high, "scalar")
        read_banks(0, range(PACK - 1))
        quantise([low], grouped[low])
        read_banks(0, [PACK - 1])
        quantise([high], grouped[high])
        for t in range(PACK):
            first_product(1, t, 1)
        first_products(2)
        read_banks(1)
        for h in range(HALVES):
            for m in EARLY:
                sums[h, m] = psum.tile([P, N], F32, name="sum%d" % (2 * h + m))
        share_h(0, N // 2)
        quantise_h(0, slice(0, N), h_grouped[0][:])

        calls, buffers = {}, {}
        start = 0
        for i in range(2, LAST + 1):
            calls[i] = []
            for count in CALLS[i]:
                calls[i].append(tuple(QUEUE[start : start + count]))
                start += count

        def scalar_pieces(i, which):
            pieces = [piece for call in calls[i] for piece in call]
            pieces = sorted(pieces, key=lambda piece: piece[0] == ("w", CHUNKS - 1))
            for piece in pieces[which]:
                call = [call for call in calls[i] if piece in call][0]
                if piece == call[0]:
                    gate = call == calls[i][-1] and i < LAST
                    buffers[call] = gate_buffer(i, 2 * K * len(call)) if gate else piece_buffer(len(call))
                k = call.index(piece)
                grouped[piece] = buffers[call][:, 2 * K * k : 2 * K * (k + 1)]
                interleave(piece, "scalar")

        ready = {TILES[0]}
        summed = []
        scalar_pieces(2, slice(0, AHEAD))
        for i in range(2, LAST + 1):
            read_banks(i, range(PACK if i < LAST else PACK - 1))
            share_h(i - 1, POOL_SHARE if i < LAST else BEFORE_LAST_SHARE)
            scalar_pieces(i, slice(AHEAD, None))
            if i < LAST:
                scalar_pieces(i + 1, slice(0, AHEAD))
            for call in calls[i][: 1 if i == LAST else None]:
                quantise(call, buffers[call][:])
                for piece in call:
                    ready.add(piece)
            quantise_h(i - 1, slice(0, N), h_grouped[i - 1][:])
            ready.add(TILES[i - 1])
            if i < LAST:
                first_products(i + 1)
            for c, h in TILES[: LAST - 1]:
                if (c, h) not in summed and (c, h) in ready and W_EARLY[c] in ready:
                    for m in EARLY:
                        second_product(c, h, m)
                    summed.append((c, h))

        read_banks(LAST, [PACK - 1])
        quantise(calls[LAST][-1], buffers[calls[LAST][-1]][:])
        quarter = N // 4
        cut = quarter + LAST_SHARE
        parts = [piece_buffer(1), gate_buffer(LAST - 1, 2 * K), piece_buffer(1)]
        interleave_h(LAST, slice(0, quarter), parts[0][:, :K], "scalar")
        interleave_h(LAST, slice(quarter, cut), parts[1][:, : PACK * LAST_SHARE], "gpsimd")
        interleave_h(LAST, slice(cut, 3 * quarter), parts[1][:, PACK * LAST_SHARE :], "scalar")
        interleave_h(LAST, slice(3 * quarter, N), parts[2][:, :K], "scalar")

        def open_late(h, m):
            sums[h, m] = psum.tile([P, N], F32, name="bank%d" % (len(LATE) * h + LATE.index(m)))
            for c in range(CHUNKS - 2):
                second_product(c, h, m)

        for m in LATE:
            open_late(0, m)
        open_late(1, LATE[0])
        for m in EARLY:
            second_product(CHUNKS - 1, 0, m)
        open_late(1, LATE[1])
        for m in LATE:
            second_product(CHUNKS - 2, 0, m)
            second_product(CHUNKS - 1, 0, m)
        second_product(CHUNKS - 2, 1, LATE[0])
        for m in EARLY:
            finish(0, m)
        quantise_h(LAST, slice(0, quarter), parts[0][:, :K])
        quantise_h(LAST, slice(quarter, 3 * quarter), parts[1][:])
        quantise_h(LAST, slice(3 * quarter, N), parts[2][:, :K])
        for m in LATE:
            finish(0, m)
        for m in EARLY:
            second_product(CHUNKS - 1, 1, m)
        second_product(CHUNKS - 2, 1, LATE[1])
        for m in LATE:
            second_product(CHUNKS - 1, 1, m)
        for m in range(PACK):
            finish(1, m)
